import numpy as np
import ml_dtypes


def mxq(x, axis, fmt="e4m3"):
    dtype, down = {"e4m3": (ml_dtypes.float8_e4m3fn, 7), "e5m2": (ml_dtypes.float8_e5m2, 14)}[fmt]
    v = np.moveaxis(np.asarray(x, np.float32).astype(ml_dtypes.bfloat16).astype(np.float64), axis, -1)
    blocks = v.reshape(v.shape[:-1] + (-1, 32))
    amax = np.abs(blocks).max(-1, keepdims=True)
    byte = np.maximum(np.where(amax > 0, np.frexp(amax)[1] - 1 + 127, 0) - down, 1)
    scale = np.exp2(byte - 127.0)
    codes = (blocks / scale).astype(np.float32).astype(dtype).astype(np.float64)
    return np.moveaxis((codes * scale).reshape(v.shape), -1, axis)


WIDE = False


def mx_kscale(k):
    if not WIDE:
        return np.ones(k)
    levels = np.array([10, -10, 5, -5, 0])
    if k % 512:
        return np.exp2(np.random.permutation(np.resize(levels, k // 32))).repeat(32)
    a = np.empty((k // 512, 16))
    for p in range(k // 512):
        a[p, :8] = np.random.permutation(np.resize(levels, 8))
        for g in range(8):
            far = levels[np.abs(levels - a[p, g]) >= 10]
            a[p, g + 8] = far[np.random.randint(len(far))]
    return np.exp2(a.ravel()).repeat(32)


BF16 = ml_dtypes.bfloat16


def bf(x):
    return np.asarray(x, np.float32).astype(BF16)


def f64(x):
    return np.asarray(x).astype(np.float64)


E2M1 = np.array([0.0, 0.5, 1.0, 1.5, 2.0, 3.0, 4.0, 6.0, -0.0, -0.5, -1.0, -1.5, -2.0, -3.0, -4.0, -6.0])


def pack_weight(w, fmt):
    k, n = w.shape
    w = f64(bf(w)).reshape(k // 32, 32, n)
    amax = np.abs(w).max(1)
    if fmt == "e4m3":
        byte = np.frexp(amax)[1] - 1 + 127 - 7
    else:
        mant, ex = np.frexp(amax / 6.0)
        byte = np.where(mant > 0.5, ex, ex - 1) + 127
    byte = np.clip(np.where(amax > 0, byte, 1), 1, 254)
    scaled = (w * np.exp2(127.0 - byte)[:, None, :]).reshape(k, n).astype(np.float32)
    by_word = np.ascontiguousarray(scaled.reshape(k // 512, 128, 4, n).transpose(0, 1, 3, 2))
    if fmt == "e4m3":
        words = by_word.astype(ml_dtypes.float8_e4m3fn).view(np.uint8)
    else:
        c = by_word.astype(ml_dtypes.float4_e2m1fn).view(np.uint8) & 0xF
        words = c[..., 0::2] | (c[..., 1::2] << 4)
    return np.ascontiguousarray(words), np.ascontiguousarray(byte.astype(np.uint8).reshape(k // 512, 16, n))


def unpack_weight(words, scales, fmt):
    g, p, n, _ = words.shape
    if fmt == "e4m3":
        vals = np.ascontiguousarray(words).view(ml_dtypes.float8_e4m3fn).astype(np.float64)
    else:
        nib = np.empty((g, p, n, 4), np.uint8)
        nib[..., 0::2] = words & 0xF
        nib[..., 1::2] = words >> 4
        vals = E2M1[nib]
    vals = vals * np.repeat(np.exp2(scales.astype(np.float64) - 127.0), 8, axis=1)[..., None]
    return vals.transpose(0, 1, 3, 2).reshape(g * 512, n)
def pack4(w):
    words, scales = pack_weight(w, "e2m1")
    return words.reshape(words.shape[0], 128, -1), scales


def unpack4(words, scales):
    return unpack_weight(words.reshape(words.shape[0], 128, -1, 2), scales, "e2m1")


def planes(Y):
    n, m = Y.shape
    b = f64(bf(Y)).reshape(n // 32, 32, m)
    amax = np.abs(b).max(1)
    byte = np.clip(np.where(amax > 0, np.frexp(amax)[1] - 1 + 127 - 7, 1), 1, 254)
    codes = (b * np.exp2(127.0 - byte)[:, None, :]).reshape(n, m).astype(np.float32).astype(ml_dtypes.float8_e4m3fn).view(np.uint8)
    words = codes.reshape(n // 512, 128, 4, m).transpose(0, 1, 3, 2)
    return np.ascontiguousarray(words), np.ascontiguousarray(byte.astype(np.uint8).reshape(n // 512, 16, m))


B, S, R, D, F, E = 4, 128, 2, 1024, 1024, 1024


def per_example_linear(inp, b, w, a):
    scaled = b[:, :, None, :] * inp[:, None, :, :]
    prod = mxq(scaled, 3, "e4m3") @ w
    return np.sum(a[:, :, None, :] * prod, axis=1)


def setup_inputs():
    s, t = mx_kscale(D), mx_kscale(F)
    x = bf(np.random.standard_normal((B, S, D)) * s)
    b1 = bf(np.random.standard_normal((B, R, D)) * 0.8)
    w1_words, w1_scales = pack4(np.random.standard_normal((D, F)) / np.sqrt(D) / s[:, None])
    a1 = bf(np.random.standard_normal((B, R, F)) * 0.8)
    b2 = bf(np.random.standard_normal((B, R, F)) * 0.8 * t)
    w2_words, w2_scales = pack4(np.random.standard_normal((F, E)) / np.sqrt(F) / t[:, None])
    a2 = bf(np.random.standard_normal((B, R, E)) * 0.8)
    return {
        "x": x,
        "b1": b1,
        "w1_words": w1_words,
        "w1_scales": w1_scales,
        "a1": a1,
        "b2": b2,
        "w2_words": w2_words,
        "w2_scales": w2_scales,
        "a2": a2,
    }


def core(x, b1, w1_words, w1_scales, a1, b2, w2_words, w2_scales, a2):
    h = np.maximum(per_example_linear(f64(x), f64(b1), unpack4(w1_words, w1_scales), f64(a1)), 0.0)
    y = per_example_linear(h, f64(b2), unpack4(w2_words, w2_scales), f64(a2))
    return y


def reference(x, b1, w1_words, w1_scales, a1, b2, w2_words, w2_scales, a2):
    R_out = core(x, b1, w1_words, w1_scales, a1, b2, w2_words, w2_scales, a2)
    words, scales = planes(np.moveaxis(R_out, 2, 0).reshape(1024, -1))
    return R_out, words, scales

@@ -1,0 +1,331 @@
+from contextlib import ExitStack
+
+import concourse.mybir as mybir
+from concourse.masks import make_identity
+
+F32 = mybir.dt.float32
+BF16 = mybir.dt.bfloat16
+I32 = mybir.dt.int32
+U32 = mybir.dt.uint32
+U8 = mybir.dt.uint8
+FP8X4 = mybir.dt.float8_e4m3fn_x4
+FP4X4 = mybir.dt.float4_e2m1fn_x4
+ALU = mybir.AluOpType
+COPY = mybir.ActivationFunctionType.Copy
+
+B, S, R, D, F, E = 4, 128, 2, 1024, 1024, 1024
+P = 128
+FLOPS = 2 * 2 * B * R * S * D * F
+
+VB1, VA1, VB2, VA2 = 0, 8, 16, 24
+
+
+def tile_floraperexampleranktworelumlp_x2_kernel(
+    tc, x, b1, w1_words, w1_scales, a1, b2, w2_words, w2_scales, a2, out_0, out_1, out_2
+):
+    nc = tc.nc
+    V, A, T, G_ = nc.vector, nc.scalar, nc.tensor, nc.gpsimd
+    with ExitStack() as ctx:
+        sb = ctx.enter_context(tc.tile_pool(name="sb", bufs=1))
+        work = ctx.enter_context(tc.tile_pool(name="work", bufs=8))
+        psum = ctx.enter_context(tc.psum_pool(name="psum", bufs=1))
+
+        def keep(shape, dtype, name):
+            return sb.tile(shape, dtype, name=name, tag=name, align_bytes=64)
+
+        def bank(kind):
+            return psum.tile([P, 512], F32, name="bank_" + kind, tag=kind, bufs=6 if kind == "mm" else 2)
+
+        ident = keep([P, P], F32, "ident")
+        vecs = keep([P, 1024], BF16, "vecs")
+        cst = keep([P, 2, 32, 4], BF16, "cst")
+        cst32 = keep([P, 2, 32, 4], F32, "cst32")
+        xs = [keep([P, 1024], BF16, "x%d" % i) for i in range(B)]
+        xT = [keep([P, 2, S, 4], BF16, "xT%d" % i) for i in range(B)]
+        w_raw = [keep([P, 2, 2048], U8, "wraw%d" % l) for l in range(2)]
+        s_raw = [keep([P, 4, 512], U8, "sraw%d" % l) for l in range(2)]
+        w_sb = [keep([P, 4, 1024], U8, "w%d" % l) for l in range(2)]
+        s_sb = [keep([P, 4, 512], U8, "s%d" % l) for l in range(2)]
+        mov = [[[keep([P, 4 * 512], BF16, "mv%d%d%d" % (l, h, g)) for g in range(2)] for h in range(2)] for l in range(2)]
+        cod = [[[keep([P, 512], U32, "cd%d%d%d" % (l, h, g)) for g in range(2)] for h in range(2)] for l in range(2)]
+        scl = [[[keep([P, 512], U8, "sc%d%d%d" % (l, h, g)) for g in range(2)] for h in range(2)] for l in range(2)]
+        res = [[[keep([P, 4, S], F32, "rs%d%d%d" % (l, i, g)) for g in range(2)] for i in range(B)] for l in range(2)]
+        yb = [[keep([P, 256 * 4], BF16, "yb%d%d" % (h, g)) for g in range(2)] for h in range(2)]
+        yc = [[keep([P, 256], U32, "yc%d%d" % (h, g)) for g in range(2)] for h in range(2)]
+        ys = [keep([P, 2, 256], U8, "ys%d" % h) for h in range(2)]
+        os_ = [[keep([P, 512], F32, "os%d%d" % (i, g)) for g in range(2)] for i in range(B)]
+
+        words = [w1_words, w2_words]
+        scales = [w1_scales, w2_scales]
+
+        def load_scales(eng, l):
+            for q in range(4):
+                eng.dma_start(
+                    out=s_raw[l][32 * q : 32 * q + 4, :, :].rearrange("p (g h) n -> p g (h n)", g=2).bitcast(I32),
+                    in_=scales[l][:, 4 * q : 4 * q + 4, :].rearrange("g r n -> r g n").bitcast(I32),
+                )
+
+        def w_perm(l, g, gg):
+            k = 2 * g + gg
+            V.tensor_copy(
+                out=w_sb[l][:, k, :].rearrange("p (t m b) -> p t m b", t=4, b=2),
+                in_=w_raw[l][:, g, 1024 * gg : 1024 * gg + 1024].rearrange("p (m t b) -> p t m b", t=4, b=2),
+            )
+
+        def s_perm(l):
+            V.tensor_copy(
+                out=s_sb[l][:].rearrange("p q (t m) -> p q t m", t=4),
+                in_=s_raw[l][:].rearrange("p q (m t) -> p q t m", t=4),
+            )
+
+        def word_transposes(src, copy_eng_fn):
+            bk = bank("tr")
+            w = src[:].bitcast(F32)
+            for g in range(2):
+                for u in range(2):
+                    T.transpose(bk[:, 128 * (2 * g + u) : 128 * (2 * g + u) + 128], w[:, 256 * g + u : 256 * g + 256 : 2], ident[:])
+            copy_eng_fn(bk[:].rearrange("p (g u s) -> p g s u", g=2, u=2))
+
+        def xm(i, g):
+            h, j = divmod(i, 2)
+            V.tensor_tensor(
+                out=mov[0][h][g][:, 1024 * j : 1024 * j + 1024].rearrange("p (r s t) -> p r s t", r=R, t=4),
+                in0=xT[i][:, g, :, :].unsqueeze(1).to_broadcast([P, R, S, 4]),
+                in1=cst[:, g, VB1 + 2 * i : VB1 + 2 * i + 2, :].unsqueeze(2).to_broadcast([P, R, S, 4]),
+                op=ALU.mult,
+            )
+
+        def quant(l, h, g):
+            V.quantize_mx(out=cod[l][h][g][:].bitcast(FP8X4), scales=scl[l][h][g][:], in_=mov[l][h][g][:])
+
+        banks = {}
+
+        def mm(l, h, gg, t, gs):
+            key = (l, h, gg, t)
+            if gs[0] == 0:
+                banks[key] = bank("mm")
+            for g in gs:
+                k = 2 * g + gg
+                T.matmul_mx(
+                    out=banks[key][:],
+                    lhsT=w_sb[l][:, k, 256 * t : 256 * t + 256].bitcast(FP4X4),
+                    lhsT_scale=s_sb[l][:, k, 128 * t : 128 * t + 128],
+                    rhs=cod[l][h][g][:].bitcast(FP8X4),
+                    rhs_scale=scl[l][h][g][:],
+                    start=(g == 0),
+                    stop=(g == 1),
+                )
+
+        tmps = {}
+
+        def col(vec, i, r, gg, t):
+            return cst32[:, gg, vec + 2 * i + r, t : t + 1]
+
+        def a_(l, h, gg, t):
+            vec = VA1 if l == 0 else VA2
+            tmp = work.tile([P, 2, S], F32, name="tmp", tag="tmp")
+            tmps[(l, h, gg, t)] = tmp
+            bk = banks[(l, h, gg, t)]
+            for j in range(2):
+                A.activation(out=tmp[:, j, :], in_=bk[:, 256 * j : 256 * j + 128], func=COPY, scale=col(vec, 2 * h + j, 0, gg, t))
+
+        def b_(l, h, gg, t):
+            vec = VA1 if l == 0 else VA2
+            bk = banks[(l, h, gg, t)]
+            tmp = tmps[(l, h, gg, t)]
+            for j in range(2):
+                V.scalar_tensor_tensor(
+                    out=res[l][2 * h + j][gg][:, t, :],
+                    in0=bk[:, 256 * j + 128 : 256 * j + 256],
+                    scalar=col(vec, 2 * h + j, 1, gg, t),
+                    in1=tmp[:, j, :],
+                    op0=ALU.mult,
+                    op1=ALU.add,
+                )
+
+        def c_(h, gg, j):
+            i = 2 * h + j
+            for r in range(R):
+                V.scalar_tensor_tensor(
+                    out=mov[1][h][gg][:, 1024 * j + 512 * r : 1024 * j + 512 * r + 512].rearrange("p (s t) -> p s t", t=4),
+                    in0=res[0][i][gg][:].rearrange("p t s -> p s t"),
+                    scalar=0.0,
+                    in1=cst32[:, gg, VB2 + 2 * i + r : VB2 + 2 * i + r + 1, :].to_broadcast([P, S, 4]),
+                    op0=ALU.max,
+                    op1=ALU.mult,
+                )
+
+        def j_(eng, h, gg, j):
+            o = yb[h][gg][:, 512 * j : 512 * j + 512].rearrange("p (s t) -> p s t", t=4)
+            s = res[1][2 * h + j][gg][:].rearrange("p t s -> p s t")
+            if eng == "v":
+                V.tensor_copy(out=o, in_=s)
+            else:
+                A.copy(out=o, in_=s)
+
+        def q3(h, gg):
+            V.quantize_mx(out=yc[h][gg][:].bitcast(FP8X4), scales=ys[h][:, gg, :], in_=yb[h][gg][:])
+            nc.sync.dma_start(
+                out=out_1[gg, :, 256 * h : 256 * h + 256, :].rearrange("p m b -> p (m b)").bitcast(I32),
+                in_=yc[h][gg][:].bitcast(I32),
+            )
+
+        def store_scales(h):
+            for q in range(4):
+                nc.sync.dma_start(
+                    out=out_2[:, 4 * q : 4 * q + 4, 256 * h : 256 * h + 256].rearrange("g q m -> q g m").bitcast(I32),
+                    in_=ys[h][32 * q : 32 * q + 4, :, :].bitcast(I32),
+                )
+
+        trb = {}
+
+        def rt(h, gg, j):
+            i = 2 * h + j
+            bk = bank("tr")
+            trb[(i, gg)] = bk
+            for t in range(4):
+                T.transpose(bk[:, 128 * t : 128 * t + 128], res[1][i][gg][:, t, :], ident[:])
+
+        def l_(eng, h, gg, j):
+            i = 2 * h + j
+            s = trb[(i, gg)][:].rearrange("s (t p) -> s p t", t=4)
+            o = os_[i][gg][:].rearrange("s (p t) -> s p t", t=4)
+            if eng == "v":
+                V.tensor_copy(out=o, in_=s)
+            else:
+                A.copy(out=o, in_=s)
+            nc.sync.dma_start(out=out_0[i, :, 512 * gg : 512 * gg + 512], in_=os_[i][gg][:])
+
+        with tc.manual_schedule():
+            G_.memset(vecs[:].bitcast(U32), 0)
+            make_identity(nc, ident[:])
+            V.memset(s_raw[0][:].bitcast(I32), 0)
+            G_.memset(s_raw[1][:].bitcast(I32), 0)
+            nc.sync.dma_start(out=xs[0][:], in_=x[0])
+            nc.scalar.dma_start(out=w_raw[0][:].bitcast(I32), in_=w1_words.rearrange("g p n -> p g n").bitcast(I32))
+            for k, v in enumerate((b1, a1, b2, a2)):
+                nc.sync.dma_start(out=vecs[8 * k : 8 * k + 8, :], in_=v.rearrange("i r d -> (i r) d"))
+            load_scales(nc.scalar, 0)
+            for i in range(1, B):
+                nc.sync.dma_start(out=xs[i][:], in_=x[i])
+            nc.sync.dma_start(out=w_raw[1][:].bitcast(I32), in_=w2_words.rearrange("g p n -> p g n").bitcast(I32))
+            load_scales(nc.sync, 1)
+
+            w_perm(0, 0, 0)
+            w_perm(0, 1, 0)
+            s_perm(0)
+
+            def copy_x(i):
+                return lambda src: A.copy(out=xT[i][:].bitcast(F32), in_=src)
+
+            def copy_c(src):
+                A.copy(out=cst[:].bitcast(F32), in_=src[:, :, 0:32, :])
+
+            word_transposes(xs[0], copy_x(0))
+            word_transposes(vecs, copy_c)
+            A.copy(out=cst32[:], in_=cst[:])
+            word_transposes(xs[1], copy_x(1))
+            xm(0, 0)
+            xm(1, 0)
+            xm(0, 1)
+            quant(0, 0, 0)
+            xm(1, 1)
+            w_perm(0, 0, 1)
+            quant(0, 0, 1)
+            w_perm(0, 1, 1)
+            word_transposes(xs[2], copy_x(2))
+            word_transposes(xs[3], copy_x(3))
+
+            both = (0, 1)
+            for t in range(4):
+                mm(0, 0, 0, t, both)
+                a_(0, 0, 0, t)
+            xm(2, 0)
+            xm(3, 0)
+            xm(2, 1)
+            quant(0, 1, 0)
+            xm(3, 1)
+            b_(0, 0, 0, 0)
+            quant(0, 1, 1)
+            for t in range(4):
+                mm(0, 0, 1, t, both)
+                a_(0, 0, 1, t)
+                if t < 3:
+                    b_(0, 0, 0, t + 1)
+            b_(0, 0, 1, 0)
+            c_(0, 0, 0)
+            b_(0, 0, 1, 1)
+            c_(0, 0, 1)
+            b_(0, 0, 1, 2)
+            b_(0, 0, 1, 3)
+            quant(1, 0, 0)
+            c_(0, 1, 0)
+            w_perm(1, 0, 0)
+            c_(0, 1, 1)
+            w_perm(1, 1, 0)
+            quant(1, 0, 1)
+            s_perm(1)
+            w_perm(1, 0, 1)
+            w_perm(1, 1, 1)
+            for gg in range(2):
+                for t in range(4):
+                    mm(0, 1, gg, t, both)
+                    a_(0, 1, gg, t)
+                    b_(0, 1, gg, t)
+                    if gg == 1 and t == 0:
+                        c_(1, 0, 0)
+                    if gg == 1 and t == 1:
+                        c_(1, 0, 1)
+                    if gg == 1 and t == 3:
+                        quant(1, 1, 0)
+            for t in range(4):
+                mm(1, 0, 0, t, both)
+                a_(1, 0, 0, t)
+            c_(1, 1, 0)
+            b_(1, 0, 0, 0)
+            c_(1, 1, 1)
+            b_(1, 0, 0, 1)
+            quant(1, 1, 1)
+            b_(1, 0, 0, 2)
+            b_(1, 0, 0, 3)
+            for t in range(4):
+                mm(1, 0, 1, t, both)
+                a_(1, 0, 1, t)
+                b_(1, 0, 1, t)
+            for j in range(2):
+                j_("a", 0, 0, j)
+            for j in range(2):
+                rt(0, 0, j)
+                l_("a", 0, 0, j)
+            for t in range(4):
+                mm(1, 1, 0, t, both)
+                a_(1, 1, 0, t)
+            q3(0, 0)
+            for t in range(4):
+                b_(1, 1, 0, t)
+            for j in range(2):
+                j_("v", 0, 1, j)
+            for j in range(2):
+                rt(0, 1, j)
+                l_("a", 0, 1, j)
+            for t in range(4):
+                mm(1, 1, 1, t, both)
+                a_(1, 1, 1, t)
+                if t == 1:
+                    q3(0, 1)
+                    store_scales(0)
+                b_(1, 1, 1, t)
+            for j in range(2):
+                j_("v", 1, 0, j)
+            for j in range(2):
+                rt(1, 0, j)
+                l_("a", 1, 0, j)
+            for j in range(2):
+                j_("v", 1, 1, j)
+            q3(1, 0)
+            for j in range(2):
+                rt(1, 1, j)
+            q3(1, 1)
+            l_("a", 1, 1, 0)
+            l_("v", 1, 1, 1)
+            store_scales(1)

@@ -11,12 +11,11 @@ U8 = mybir.dt.uint8
 FP8X4 = mybir.dt.float8_e4m3fn_x4
 FP4X4 = mybir.dt.float4_e2m1fn_x4
 ALU = mybir.AluOpType
-COPY = mybir.ActivationFunctionType.Copy
+ACT = mybir.ActivationFunctionType
 
 B, S, R, D, F, E = 4, 128, 2, 1024, 1024, 1024
 P = 128
 FLOPS = 2 * 2 * B * R * S * D * F
-
 VB1, VA1, VB2, VA2 = 0, 8, 16, 24
 
 
@@ -27,76 +26,124 @@ def tile_floraperexampleranktworelumlp_x2_kernel(
     V, A, T, G_ = nc.vector, nc.scalar, nc.tensor, nc.gpsimd
     with ExitStack() as ctx:
         sb = ctx.enter_context(tc.tile_pool(name="sb", bufs=1))
-        work = ctx.enter_context(tc.tile_pool(name="work", bufs=8))
         psum = ctx.enter_context(tc.psum_pool(name="psum", bufs=1))
+        made = {}
 
         def keep(shape, dtype, name):
-            return sb.tile(shape, dtype, name=name, tag=name, align_bytes=64)
+            if name not in made:
+                made[name] = sb.tile(shape, dtype, name=name, tag=name, align_bytes=64)
+            return made[name]
+
+        def ring(shape, dtype, tag, bufs):
+            return sb.tile(shape, dtype, name=tag, tag=tag, bufs=bufs, align_bytes=64)
 
         def bank(kind):
-            return psum.tile([P, 512], F32, name="bank_" + kind, tag=kind, bufs=6 if kind == "mm" else 2)
+            return psum.tile([P, 512], F32, name="bank", tag="bank", bufs=7)
 
         ident = keep([P, P], F32, "ident")
+        ident_bf = keep([P, P], BF16, "identbf")
+        cps = psum.tile([P, 256], BF16, name="cps", tag="cps", bufs=1)
+        cpv = cps[:].rearrange("p (g r t) -> p g r t", g=2, t=4)
         vecs = keep([P, 1024], BF16, "vecs")
         cst = keep([P, 2, 32, 4], BF16, "cst")
         cst32 = keep([P, 2, 32, 4], F32, "cst32")
         xs = [keep([P, 1024], BF16, "x%d" % i) for i in range(B)]
         xT = [keep([P, 2, S, 4], BF16, "xT%d" % i) for i in range(B)]
         w_raw = [keep([P, 2, 2048], U8, "wraw%d" % l) for l in range(2)]
-        s_raw = [keep([P, 4, 512], U8, "sraw%d" % l) for l in range(2)]
+        s_raw = keep([P, 2, 1024], U8, "sraw")
         w_sb = [keep([P, 4, 1024], U8, "w%d" % l) for l in range(2)]
         s_sb = [keep([P, 4, 512], U8, "s%d" % l) for l in range(2)]
-        mov = [[[keep([P, 4 * 512], BF16, "mv%d%d%d" % (l, h, g)) for g in range(2)] for h in range(2)] for l in range(2)]
-        cod = [[[keep([P, 512], U32, "cd%d%d%d" % (l, h, g)) for g in range(2)] for h in range(2)] for l in range(2)]
-        scl = [[[keep([P, 512], U8, "sc%d%d%d" % (l, h, g)) for g in range(2)] for h in range(2)] for l in range(2)]
-        res = [[[keep([P, 4, S], F32, "rs%d%d%d" % (l, i, g)) for g in range(2)] for i in range(B)] for l in range(2)]
-        yb = [[keep([P, 256 * 4], BF16, "yb%d%d" % (h, g)) for g in range(2)] for h in range(2)]
-        yc = [[keep([P, 256], U32, "yc%d%d" % (h, g)) for g in range(2)] for h in range(2)]
-        ys = [keep([P, 2, 256], U8, "ys%d" % h) for h in range(2)]
-        os_ = [[keep([P, 512], F32, "os%d%d" % (i, g)) for g in range(2)] for i in range(B)]
-
         words = [w1_words, w2_words]
         scales = [w1_scales, w2_scales]
+
+        def mov(l, h, g):
+            return keep([P, 2048], BF16, "mv%d%d%d" % (l, h, g))
+
+        def cod(l, h, g):
+            return keep([P, 512], U32, "cd%d%d%d" % (l, h, g))
+
+        def scl(l, h, g):
+            return keep([P, 512], U8, "sc%d%d%d" % (l, h, g))
+
+        def res(l, h, g):
+            return keep([P, 2, 4, S], F32, "rs%d%d%d" % (l, h, g))
 
         def load_scales(eng, l):
             for q in range(4):
                 eng.dma_start(
-                    out=s_raw[l][32 * q : 32 * q + 4, :, :].rearrange("p (g h) n -> p g (h n)", g=2).bitcast(I32),
+                    out=s_raw[32 * q + 4 * l : 32 * q + 4 * l + 4, :, :].bitcast(I32),
                     in_=scales[l][:, 4 * q : 4 * q + 4, :].rearrange("g r n -> r g n").bitcast(I32),
                 )
 
-        def w_perm(l, g, gg):
-            k = 2 * g + gg
-            V.tensor_copy(
-                out=w_sb[l][:, k, :].rearrange("p (t m b) -> p t m b", t=4, b=2),
-                in_=w_raw[l][:, g, 1024 * gg : 1024 * gg + 1024].rearrange("p (m t b) -> p t m b", t=4, b=2),
+        def w_load(eng, l, gg):
+            eng.dma_start(
+                out=w_raw[l][:, :, 1024 * gg : 1024 * gg + 1024].bitcast(I32),
+                in_=words[l][:, :, 1024 * gg : 1024 * gg + 1024].rearrange("g p n -> p g n").bitcast(I32),
             )
 
-        def s_perm(l):
-            V.tensor_copy(
-                out=s_sb[l][:].rearrange("p q (t m) -> p q t m", t=4),
-                in_=s_raw[l][:].rearrange("p q (m t) -> p q t m", t=4),
-            )
+        def w_perm(eng, l, g, gg):
+            o = w_sb[l][:, 2 * g + gg, :].rearrange("p (t m b) -> p t m b", t=4, b=2)
+            s = w_raw[l][:, g, 1024 * gg : 1024 * gg + 1024].rearrange("p (m t b) -> p t m b", t=4, b=2)
+            if eng == "v":
+                V.tensor_copy(out=o, in_=s)
+            else:
+                for z in range(2):
+                    G_.tensor_copy(out=o[:, 2 * z : 2 * z + 2], in_=s[:, 2 * z : 2 * z + 2])
 
-        def word_transposes(src, copy_eng_fn):
+        def s_perm():
+            V.tensor_copy(
+                out=s_sb[0][:].rearrange("p q (t m) -> p q t m", t=4),
+                in_=s_raw[:].rearrange("p g (h m t) -> p (g h) t m", t=4, h=2),
+            )
+            for q in range(4):
+                nc.sync.dma_start(
+                    out=s_sb[1][32 * q : 32 * q + 4, :, :].bitcast(I32),
+                    in_=s_sb[0][32 * q + 4 : 32 * q + 8, :, :].bitcast(I32),
+                )
+
+        def word_transposes(src):
             bk = bank("tr")
             w = src[:].bitcast(F32)
             for g in range(2):
                 for u in range(2):
-                    T.transpose(bk[:, 128 * (2 * g + u) : 128 * (2 * g + u) + 128], w[:, 256 * g + u : 256 * g + 256 : 2], ident[:])
-            copy_eng_fn(bk[:].rearrange("p (g u s) -> p g s u", g=2, u=2))
+                    T.transpose(
+                        bk[:, 128 * (2 * g + u) : 128 * (2 * g + u) + 128], w[:, 256 * g + u : 256 * g + 256 : 2], ident[:]
+                    )
+            return bk[:].rearrange("p (g u s) -> p g s u", g=2, u=2)
+
+        def xT_load(i):
+            A.copy(out=xT[i][:].bitcast(F32), in_=word_transposes(xs[i]))
+
+        def consts():
+            A.copy(out=cst[:].bitcast(F32), in_=word_transposes(vecs)[:, :, 0:32, :])
+
+        def consts2():
+            A.copy(out=cst32[:], in_=cst[:])
+            T.matmul(out=cps[:], lhsT=ident_bf[:], rhs=cst[:].rearrange("p g r t -> p (g r t)"), start=True, stop=True)
 
         def xm(i, g):
             h, j = divmod(i, 2)
             V.tensor_tensor(
-                out=mov[0][h][g][:, 1024 * j : 1024 * j + 1024].rearrange("p (r s t) -> p r s t", r=R, t=4),
+                out=mov(0, h, g)[:, 1024 * j : 1024 * j + 1024].rearrange("p (r s t) -> p r s t", r=R, t=4),
                 in0=xT[i][:, g, :, :].unsqueeze(1).to_broadcast([P, R, S, 4]),
-                in1=cst[:, g, VB1 + 2 * i : VB1 + 2 * i + 2, :].unsqueeze(2).to_broadcast([P, R, S, 4]),
+                in1=cpv[:, g, VB1 + 2 * i : VB1 + 2 * i + 2, :].unsqueeze(2).to_broadcast([P, R, S, 4]),
                 op=ALU.mult,
             )
 
+        def xg(i, g):
+            h, j = divmod(i, 2)
+            for r in range(2):
+                for z in range(2):
+                    o = 1024 * j + 512 * r + 256 * z
+                    G_.tensor_tensor(
+                        out=mov(0, h, g)[:, o : o + 256].rearrange("p (s t) -> p s t", t=4),
+                        in0=xT[i][:, g, 64 * z : 64 * z + 64, :],
+                        in1=cst[:, g, VB1 + 2 * i + r : VB1 + 2 * i + r + 1, :].to_broadcast([P, 64, 4]),
+                        op=ALU.mult,
+                    )
+
         def quant(l, h, g):
-            V.quantize_mx(out=cod[l][h][g][:].bitcast(FP8X4), scales=scl[l][h][g][:], in_=mov[l][h][g][:])
+            V.quantize_mx(out=cod(l, h, g)[:].bitcast(FP8X4), scales=scl(l, h, g)[:], in_=mov(l, h, g)[:])
 
         banks = {}
 
@@ -110,8 +157,8 @@ def tile_floraperexampleranktworelumlp_x2_kernel(
                     out=banks[key][:],
                     lhsT=w_sb[l][:, k, 256 * t : 256 * t + 256].bitcast(FP4X4),
                     lhsT_scale=s_sb[l][:, k, 128 * t : 128 * t + 128],
-                    rhs=cod[l][h][g][:].bitcast(FP8X4),
-                    rhs_scale=scl[l][h][g][:],
+                    rhs=cod(l, h, g)[:].bitcast(FP8X4),
+                    rhs_scale=scl(l, h, g)[:],
                     start=(g == 0),
                     stop=(g == 1),
                 )
@@ -121,211 +168,349 @@ def tile_floraperexampleranktworelumlp_x2_kernel(
         def col(vec, i, r, gg, t):
             return cst32[:, gg, vec + 2 * i + r, t : t + 1]
 
-        def a_(l, h, gg, t):
-            vec = VA1 if l == 0 else VA2
-            tmp = work.tile([P, 2, S], F32, name="tmp", tag="tmp")
-            tmps[(l, h, gg, t)] = tmp
+        def scaled(l, h, gg, t, r, tag, bufs):
+            tmp = ring([P, 2, S], F32, tag, bufs)
             bk = banks[(l, h, gg, t)]
             for j in range(2):
-                A.activation(out=tmp[:, j, :], in_=bk[:, 256 * j : 256 * j + 128], func=COPY, scale=col(vec, 2 * h + j, 0, gg, t))
+                A.activation(
+                    out=tmp[:, j, :],
+                    in_=bk[:, 256 * j + 128 * r : 256 * j + 128 * r + 128],
+                    func=ACT.Copy,
+                    scale=col(VA1 if l == 0 else VA2, 2 * h + j, r, gg, t),
+                )
+            return tmp
+
+        def a_(l, h, gg, t):
+            tmps[(l, h, gg, t)] = scaled(l, h, gg, t, 0, "tmp", 16)
 
         def b_(l, h, gg, t):
-            vec = VA1 if l == 0 else VA2
-            bk = banks[(l, h, gg, t)]
-            tmp = tmps[(l, h, gg, t)]
             for j in range(2):
                 V.scalar_tensor_tensor(
-                    out=res[l][2 * h + j][gg][:, t, :],
-                    in0=bk[:, 256 * j + 128 : 256 * j + 256],
-                    scalar=col(vec, 2 * h + j, 1, gg, t),
-                    in1=tmp[:, j, :],
+                    out=res(l, h, gg)[:, j, t, :],
+                    in0=banks[(l, h, gg, t)][:, 256 * j + 128 : 256 * j + 256],
+                    scalar=col(VA1 if l == 0 else VA2, 2 * h + j, 1, gg, t),
+                    in1=tmps[(l, h, gg, t)][:, j, :],
                     op0=ALU.mult,
                     op1=ALU.add,
                 )
 
-        def c_(h, gg, j):
-            i = 2 * h + j
-            for r in range(R):
-                V.scalar_tensor_tensor(
-                    out=mov[1][h][gg][:, 1024 * j + 512 * r : 1024 * j + 512 * r + 512].rearrange("p (s t) -> p s t", t=4),
-                    in0=res[0][i][gg][:].rearrange("p t s -> p s t"),
-                    scalar=0.0,
-                    in1=cst32[:, gg, VB2 + 2 * i + r : VB2 + 2 * i + r + 1, :].to_broadcast([P, S, 4]),
+        def bg_(l, h, gg, t):
+            tm1 = scaled(l, h, gg, t, 1, "tm1", 8)
+            G_.tensor_tensor(out=res(l, h, gg)[:, :, t, :], in0=tmps[(l, h, gg, t)][:], in1=tm1[:], op=ALU.add)
+
+        def mv1(h, gg, j, r):
+            o = 1024 * j + 512 * r
+            return mov(1, h, gg)[:, o : o + 512].rearrange("p (s t) -> p s t", t=4)
+
+        def cr(h, gg, j, r):
+            row = VB2 + 2 * (2 * h + j) + r
+            V.scalar_tensor_tensor(
+                out=mv1(h, gg, j, r),
+                in0=res(0, h, gg)[:, j, :, :].rearrange("p t s -> p s t"),
+                scalar=0.0,
+                in1=cpv[:, gg, row : row + 1, :].to_broadcast([P, S, 4]),
+                op0=ALU.max,
+                op1=ALU.mult,
+            )
+
+        def cx(h, gg, j, r):
+            pl = keep([P, 4, S], BF16, "pl%d%d%d%d" % (h, gg, j, r))
+            for t in range(4):
+                V.tensor_scalar(
+                    out=pl[:, t, :],
+                    in0=res(0, h, gg)[:, j, t, :],
+                    scalar1=0.0,
+                    scalar2=col(VB2, 2 * h + j, r, gg, t),
                     op0=ALU.max,
                     op1=ALU.mult,
                 )
+            A.copy(out=mv1(h, gg, j, r), in_=pl[:].rearrange("p t s -> p s t"))
+
+        def cg1(h, gg, j, r):
+            name = "hi%d%d%d" % (h, gg, j)
+            new = name not in made
+            hi = keep([P, S, 4], F32, name)
+            if new:
+                A.activation(out=hi[:], in_=res(0, h, gg)[:, j, :, :].rearrange("p t s -> p s t"), func=ACT.Relu)
+            row = VB2 + 2 * (2 * h + j) + r
+            for z in range(2):
+                G_.tensor_tensor(
+                    out=mv1(h, gg, j, r)[:, 64 * z : 64 * z + 64, :],
+                    in0=hi[:, 64 * z : 64 * z + 64, :],
+                    in1=cst32[:, gg, row : row + 1, :].to_broadcast([P, 64, 4]),
+                    op=ALU.mult,
+                )
+
+        def yb(h, gg):
+            return keep([P, 1024], BF16, "yb%d%d" % (h, gg))
+
+        def ys(h):
+            return keep([P, 2, 256], U8, "ys%d" % h)
 
         def j_(eng, h, gg, j):
-            o = yb[h][gg][:, 512 * j : 512 * j + 512].rearrange("p (s t) -> p s t", t=4)
-            s = res[1][2 * h + j][gg][:].rearrange("p t s -> p s t")
+            o = yb(h, gg)[:, 512 * j : 512 * j + 512].rearrange("p (s t) -> p s t", t=4)
+            s = res(1, h, gg)[:, j, :, :].rearrange("p t s -> p s t")
             if eng == "v":
                 V.tensor_copy(out=o, in_=s)
+            elif eng == "g":
+                G_.tensor_scalar(out=o, in0=s, scalar1=1.0, scalar2=1.0, op0=ALU.mult, op1=ALU.mult)
             else:
                 A.copy(out=o, in_=s)
 
         def q3(h, gg):
-            V.quantize_mx(out=yc[h][gg][:].bitcast(FP8X4), scales=ys[h][:, gg, :], in_=yb[h][gg][:])
+            yc = keep([P, 256], U32, "yc%d%d" % (h, gg))
+            V.quantize_mx(out=yc[:].bitcast(FP8X4), scales=ys(h)[:, gg, :], in_=yb(h, gg)[:])
             nc.sync.dma_start(
                 out=out_1[gg, :, 256 * h : 256 * h + 256, :].rearrange("p m b -> p (m b)").bitcast(I32),
-                in_=yc[h][gg][:].bitcast(I32),
+                in_=yc[:].bitcast(I32),
             )
 
         def store_scales(h):
             for q in range(4):
                 nc.sync.dma_start(
                     out=out_2[:, 4 * q : 4 * q + 4, 256 * h : 256 * h + 256].rearrange("g q m -> q g m").bitcast(I32),
-                    in_=ys[h][32 * q : 32 * q + 4, :, :].bitcast(I32),
+                    in_=ys(h)[32 * q : 32 * q + 4, :, :].bitcast(I32),
                 )
 
         trb = {}
 
-        def rt(h, gg, j):
-            i = 2 * h + j
-            bk = bank("tr")
-            trb[(i, gg)] = bk
+        def rt(h, gg, j, kind="tr"):
+            bk = bank(kind)
+            trb[(h, gg, j)] = bk
             for t in range(4):
-                T.transpose(bk[:, 128 * t : 128 * t + 128], res[1][i][gg][:, t, :], ident[:])
+                T.transpose(bk[:, 128 * t : 128 * t + 128], res(1, h, gg)[:, j, t, :], ident[:])
 
         def l_(eng, h, gg, j):
-            i = 2 * h + j
-            s = trb[(i, gg)][:].rearrange("s (t p) -> s p t", t=4)
-            o = os_[i][gg][:].rearrange("s (p t) -> s p t", t=4)
+            ot = keep([P, 512], F32, "os%d%d%d" % (h, gg, j))
+            s = trb[(h, gg, j)][:].rearrange("s (t p) -> s p t", t=4)
+            o = ot[:].rearrange("s (p t) -> s p t", t=4)
             if eng == "v":
                 V.tensor_copy(out=o, in_=s)
             else:
                 A.copy(out=o, in_=s)
-            nc.sync.dma_start(out=out_0[i, :, 512 * gg : 512 * gg + 512], in_=os_[i][gg][:])
+            nc.sync.dma_start(out=out_0[2 * h + j, :, 512 * gg : 512 * gg + 512], in_=ot[:])
 
         with tc.manual_schedule():
-            G_.memset(vecs[:].bitcast(U32), 0)
+            G_.memset(vecs[32:64, :].bitcast(U32), 0)
+            G_.memset(vecs[64:128, :].bitcast(U32), 0)
+            V.memset(s_raw[:].bitcast(I32), 0)
             make_identity(nc, ident[:])
-            V.memset(s_raw[0][:].bitcast(I32), 0)
-            G_.memset(s_raw[1][:].bitcast(I32), 0)
+            G_.memset(s_sb[1][:].bitcast(I32), 0)
+            w_load(nc.scalar, 0, 0)
+            A.copy(out=ident_bf[:], in_=ident[:])
             nc.sync.dma_start(out=xs[0][:], in_=x[0])
-            nc.scalar.dma_start(out=w_raw[0][:].bitcast(I32), in_=w1_words.rearrange("g p n -> p g n").bitcast(I32))
             for k, v in enumerate((b1, a1, b2, a2)):
                 nc.sync.dma_start(out=vecs[8 * k : 8 * k + 8, :], in_=v.rearrange("i r d -> (i r) d"))
-            load_scales(nc.scalar, 0)
-            for i in range(1, B):
-                nc.sync.dma_start(out=xs[i][:], in_=x[i])
-            nc.sync.dma_start(out=w_raw[1][:].bitcast(I32), in_=w2_words.rearrange("g p n -> p g n").bitcast(I32))
+            w_load(nc.sync, 0, 1)
+            nc.sync.dma_start(out=xs[1][:], in_=x[1])
+            load_scales(nc.sync, 0)
             load_scales(nc.sync, 1)
-
-            w_perm(0, 0, 0)
-            w_perm(0, 1, 0)
-            s_perm(0)
-
-            def copy_x(i):
-                return lambda src: A.copy(out=xT[i][:].bitcast(F32), in_=src)
-
-            def copy_c(src):
-                A.copy(out=cst[:].bitcast(F32), in_=src[:, :, 0:32, :])
-
-            word_transposes(xs[0], copy_x(0))
-            word_transposes(vecs, copy_c)
-            A.copy(out=cst32[:], in_=cst[:])
-            word_transposes(xs[1], copy_x(1))
-            xm(0, 0)
-            xm(1, 0)
-            xm(0, 1)
-            quant(0, 0, 0)
-            xm(1, 1)
-            w_perm(0, 0, 1)
-            quant(0, 0, 1)
-            w_perm(0, 1, 1)
-            word_transposes(xs[2], copy_x(2))
-            word_transposes(xs[3], copy_x(3))
-
-            both = (0, 1)
-            for t in range(4):
-                mm(0, 0, 0, t, both)
-                a_(0, 0, 0, t)
-            xm(2, 0)
-            xm(3, 0)
-            xm(2, 1)
-            quant(0, 1, 0)
-            xm(3, 1)
-            b_(0, 0, 0, 0)
-            quant(0, 1, 1)
-            for t in range(4):
-                mm(0, 0, 1, t, both)
-                a_(0, 0, 1, t)
-                if t < 3:
-                    b_(0, 0, 0, t + 1)
-            b_(0, 0, 1, 0)
-            c_(0, 0, 0)
-            b_(0, 0, 1, 1)
-            c_(0, 0, 1)
-            b_(0, 0, 1, 2)
-            b_(0, 0, 1, 3)
-            quant(1, 0, 0)
-            c_(0, 1, 0)
-            w_perm(1, 0, 0)
-            c_(0, 1, 1)
-            w_perm(1, 1, 0)
-            quant(1, 0, 1)
-            s_perm(1)
-            w_perm(1, 0, 1)
-            w_perm(1, 1, 1)
-            for gg in range(2):
-                for t in range(4):
-                    mm(0, 1, gg, t, both)
-                    a_(0, 1, gg, t)
-                    b_(0, 1, gg, t)
-                    if gg == 1 and t == 0:
-                        c_(1, 0, 0)
-                    if gg == 1 and t == 1:
-                        c_(1, 0, 1)
-                    if gg == 1 and t == 3:
-                        quant(1, 1, 0)
-            for t in range(4):
-                mm(1, 0, 0, t, both)
-                a_(1, 0, 0, t)
-            c_(1, 1, 0)
-            b_(1, 0, 0, 0)
-            c_(1, 1, 1)
-            b_(1, 0, 0, 1)
-            quant(1, 1, 1)
-            b_(1, 0, 0, 2)
-            b_(1, 0, 0, 3)
-            for t in range(4):
-                mm(1, 0, 1, t, both)
-                a_(1, 0, 1, t)
-                b_(1, 0, 1, t)
-            for j in range(2):
-                j_("a", 0, 0, j)
-            for j in range(2):
-                rt(0, 0, j)
-                l_("a", 0, 0, j)
-            for t in range(4):
-                mm(1, 1, 0, t, both)
-                a_(1, 1, 0, t)
-            q3(0, 0)
-            for t in range(4):
-                b_(1, 1, 0, t)
-            for j in range(2):
-                j_("v", 0, 1, j)
-            for j in range(2):
-                rt(0, 1, j)
-                l_("a", 0, 1, j)
-            for t in range(4):
-                mm(1, 1, 1, t, both)
-                a_(1, 1, 1, t)
-                if t == 1:
-                    q3(0, 1)
-                    store_scales(0)
-                b_(1, 1, 1, t)
-            for j in range(2):
-                j_("v", 1, 0, j)
-            for j in range(2):
-                rt(1, 0, j)
-                l_("a", 1, 0, j)
-            for j in range(2):
-                j_("v", 1, 1, j)
-            q3(1, 0)
-            for j in range(2):
-                rt(1, 1, j)
-            q3(1, 1)
-            l_("a", 1, 1, 0)
-            l_("v", 1, 1, 1)
+            nc.sync.dma_start(out=xs[2][:], in_=x[2])
+            nc.sync.dma_start(out=xs[3][:], in_=x[3])
+            w_load(nc.sync, 1, 0)
+            w_load(nc.sync, 1, 1)
+            xT_load(0)
+            w_perm('v',0,1,0)
+            consts()
+            xT_load(1)
+            consts2()
+            w_perm('v',0,0,0)
+            xm(0,1)
+            xm(1,1)
+            s_perm()
+            xm(1,0)
+            xT_load(2)
+            xm(0,0)
+            xm(2,1)
+            xT_load(3)
+            w_perm('g',0,1,1)
+            w_perm('g',0,0,1)
+            xm(3,1)
+            quant(0,0,0)
+            xm(2,0)
+            mm(0,0,1,0,(0,))
+            mm(0,0,1,2,(0,))
+            mm(0,0,1,1,(0,))
+            quant(0,0,1)
+            w_perm('g',1,0,0)
+            mm(0,0,1,0,(1,))
+            mm(0,0,1,2,(1,))
+            xm(3,0)
+            a_(0,0,1,2)
+            mm(0,0,1,3,(0,))
+            mm(0,0,0,1,(0,))
+            mm(0,0,1,3,(1,))
+            quant(0,1,1)
+            quant(0,1,0)
+            mm(0,0,0,0,(0,))
+            mm(0,0,1,1,(1,))
+            mm(0,1,0,0,(0,))
+            a_(0,0,1,0)
+            mm(0,1,0,0,(1,))
+            mm(0,0,0,1,(1,))
+            a_(0,0,1,3)
+            a_(0,0,1,1)
+            b_(0,0,1,0)
+            w_perm('v',1,1,1)
+            b_(0,0,1,2)
+            mm(0,0,0,0,(1,))
+            a_(0,0,0,1)
+            mm(0,1,1,2,(0,))
+            b_(0,0,1,3)
+            mm(0,1,0,1,(0,))
+            a_(0,1,0,0)
+            b_(0,0,1,1)
+            mm(0,1,0,3,(0,))
+            cr(0,1,0,0)
+            mm(0,0,0,3,(0,))
+            mm(0,0,0,3,(1,))
+            mm(0,0,0,2,(0,))
+            a_(0,0,0,0)
+            b_(0,0,0,1)
+            mm(0,1,0,1,(1,))
+            w_perm('v',1,1,0)
+            mm(0,0,0,2,(1,))
+            cg1(0,1,0,1)
+            mm(0,1,0,2,(0,))
+            a_(0,0,0,3)
+            b_(0,1,0,0)
+            a_(0,0,0,2)
+            b_(0,0,0,3)
+            b_(0,0,0,0)
+            mm(0,1,1,1,(0,))
+            b_(0,0,0,2)
+            cg1(0,1,1,0)
+            mm(0,1,0,2,(1,))
+            cx(0,1,1,1)
+            mm(0,1,1,0,(0,))
+            mm(0,1,1,1,(1,))
+            mm(0,1,1,3,(0,))
+            mm(0,1,1,0,(1,))
+            cr(0,0,0,0)
+            mm(0,1,0,3,(1,))
+            cr(0,0,1,1)
+            a_(0,1,0,2)
+            cr(0,0,1,0)
+            a_(0,1,0,3)
+            b_(0,1,0,3)
+            mm(0,1,1,3,(1,))
+            b_(0,1,0,2)
+            mm(0,1,1,2,(1,))
+            cr(0,0,0,1)
+            a_(0,1,0,1)
+            b_(0,1,0,1)
+            w_perm('g',1,0,1)
+            a_(0,1,1,3)
+            quant(1,0,0)
+            quant(1,0,1)
+            a_(0,1,1,1)
+            a_(0,1,1,2)
+            mm(1,0,1,0,(0,))
+            mm(1,0,0,0,(0,))
+            a_(0,1,1,0)
+            mm(1,0,0,0,(1,))
+            cg1(1,0,0,1)
+            mm(1,0,0,1,(0,))
+            mm(1,0,0,1,(1,))
+            b_(0,1,1,1)
+            b_(0,1,1,3)
+            mm(1,0,0,2,(0,))
+            cr(1,0,1,1)
+            a_(1,0,0,0)
+            mm(1,0,1,2,(0,))
+            bg_(1,0,0,0)
+            cr(1,0,1,0)
+            mm(1,0,0,2,(1,))
+            mm(1,0,1,1,(0,))
+            mm(1,0,1,1,(1,))
+            mm(1,0,0,3,(0,))
+            a_(1,0,0,1)
+            cr(1,0,0,0)
+            a_(1,0,0,2)
+            bg_(1,0,0,1)
+            mm(1,0,1,0,(1,))
+            b_(0,1,1,2)
+            quant(1,1,0)
+            a_(1,0,1,1)
+            a_(1,0,1,0)
+            mm(1,0,0,3,(1,))
+            bg_(1,0,0,2)
+            mm(1,0,1,2,(1,))
+            mm(1,0,1,3,(0,))
+            a_(1,0,0,3)
+            mm(1,1,0,0,(0,))
+            mm(1,1,0,3,(0,))
+            mm(1,0,1,3,(1,))
+            bg_(1,0,0,3)
+            rt(0,0,0)
+            rt(0,0,1)
+            bg_(1,0,1,1)
+            mm(1,1,1,0,(0,))
+            a_(1,0,1,2)
+            a_(1,0,1,3)
+            mm(1,1,0,2,(0,))
+            b_(0,1,1,0)
+            cr(1,1,0,0)
+            bg_(1,0,1,2)
+            cr(1,1,1,1)
+            bg_(1,0,1,0)
+            bg_(1,0,1,3)
+            cr(1,1,1,0)
+            cr(1,1,0,1)
+            quant(1,1,1)
+            l_('v',0,0,0)
+            mm(1,1,1,1,(0,))
+            mm(1,1,1,0,(1,))
+            mm(1,1,0,0,(1,))
+            j_('g',0,1,0)
+            mm(1,1,0,2,(1,))
+            mm(1,1,0,1,(0,))
+            l_('a',0,0,1)
+            j_('a',0,0,1)
+            a_(1,1,1,0)
+            mm(1,1,0,3,(1,))
+            a_(1,1,0,2)
+            j_('a',0,0,0)
+            b_(1,1,0,2)
+            a_(1,1,0,0)
+            rt(0,1,0)
+            mm(1,1,0,1,(1,))
+            j_('g',0,1,1)
+            mm(1,1,1,2,(0,))
+            a_(1,1,0,3)
+            l_('v',0,1,0)
+            b_(1,1,0,0)
+            mm(1,1,1,1,(1,))
+            mm(1,1,1,2,(1,))
+            q3(0,0)
+            b_(1,1,0,3)
+            a_(1,1,0,1)
+            a_(1,1,1,1)
+            b_(1,1,0,1)
+            mm(1,1,1,3,(0,))
+            j_('g',1,0,1)
+            a_(1,1,1,2)
+            mm(1,1,1,3,(1,))
+            rt(0,1,1)
+            q3(0,1)
+            b_(1,1,1,2)
+            rt(1,0,1,'mm')
+            rt(1,0,0,'mm')
+            a_(1,1,1,3)
+            l_('a',0,1,1)
+            l_('a',1,0,1)
+            store_scales(0)
+            l_('a',1,0,0)
+            b_(1,1,1,1)
+            b_(1,1,1,3)
+            b_(1,1,1,0)
+            j_('g',1,1,1)
+            rt(1,1,0)
+            j_('g',1,1,0)
+            j_('a',1,0,0)
+            l_('v',1,1,0)
+            rt(1,1,1)
+            l_('v',1,1,1)
+            q3(1,0)
+            q3(1,1)
             store_scales(1)

@@ -38,21 +38,20 @@ def tile_floraperexampleranktworelumlp_x2_kernel(
             return sb.tile(shape, dtype, name=tag, tag=tag, bufs=bufs, align_bytes=64)
 
         def bank(kind):
-            return psum.tile([P, 512], F32, name="bank", tag="bank", bufs=7)
+            return psum.tile([P, 512], F32, name="bank", tag="bank", bufs=8)
 
         ident = keep([P, P], F32, "ident")
         ident_bf = keep([P, P], BF16, "identbf")
-        cps = psum.tile([P, 256], BF16, name="cps", tag="cps", bufs=1)
-        cpv = cps[:].rearrange("p (g r t) -> p g r t", g=2, t=4)
+        cn32 = keep([P, 8, 8], F32, "cn32")
         vecs = keep([P, 1024], BF16, "vecs")
         cst = keep([P, 2, 32, 4], BF16, "cst")
         cst32 = keep([P, 2, 32, 4], F32, "cst32")
         xs = [keep([P, 1024], BF16, "x%d" % i) for i in range(B)]
         xT = [keep([P, 2, S, 4], BF16, "xT%d" % i) for i in range(B)]
         w_raw = [keep([P, 2, 2048], U8, "wraw%d" % l) for l in range(2)]
-        s_raw = keep([P, 2, 1024], U8, "sraw")
-        w_sb = [keep([P, 4, 1024], U8, "w%d" % l) for l in range(2)]
-        s_sb = [keep([P, 4, 512], U8, "s%d" % l) for l in range(2)]
+        s_raw = keep([P, 2048], U8, "sraw")
+        w_sb = keep([P, 4, 1024], U8, "w1p")
+        s_sb = [keep([P, 2048], U8, "s%d" % l) for l in range(2)]
         words = [w1_words, w2_words]
         scales = [w1_scales, w2_scales]
 
@@ -68,10 +67,10 @@ def tile_floraperexampleranktworelumlp_x2_kernel(
         def res(l, h, g):
             return keep([P, 2, 4, S], F32, "rs%d%d%d" % (l, h, g))
 
-        def load_scales(eng, l):
+        def load_scales(eng, l, dst):
             for q in range(4):
                 eng.dma_start(
-                    out=s_raw[32 * q + 4 * l : 32 * q + 4 * l + 4, :, :].bitcast(I32),
+                    out=dst[32 * q : 32 * q + 4, :].bitcast(I32).rearrange("p (g n) -> p g n", g=2),
                     in_=scales[l][:, 4 * q : 4 * q + 4, :].rearrange("g r n -> r g n").bitcast(I32),
                 )
 
@@ -82,7 +81,7 @@ def tile_floraperexampleranktworelumlp_x2_kernel(
             )
 
         def w_perm(eng, l, g, gg):
-            o = w_sb[l][:, 2 * g + gg, :].rearrange("p (t m b) -> p t m b", t=4, b=2)
+            o = w_sb[:, 2 * g + gg, :].rearrange("p (t m b) -> p t m b", t=4, b=2)
             s = w_raw[l][:, g, 1024 * gg : 1024 * gg + 1024].rearrange("p (m t b) -> p t m b", t=4, b=2)
             if eng == "v":
                 V.tensor_copy(out=o, in_=s)
@@ -92,14 +91,9 @@ def tile_floraperexampleranktworelumlp_x2_kernel(
 
         def s_perm():
             V.tensor_copy(
-                out=s_sb[0][:].rearrange("p q (t m) -> p q t m", t=4),
-                in_=s_raw[:].rearrange("p g (h m t) -> p (g h) t m", t=4, h=2),
+                out=s_sb[0][:].rearrange("p (q t m) -> p q t m", q=4, t=4),
+                in_=s_raw[:].rearrange("p (q m t) -> p q t m", q=4, t=4),
             )
-            for q in range(4):
-                nc.sync.dma_start(
-                    out=s_sb[1][32 * q : 32 * q + 4, :, :].bitcast(I32),
-                    in_=s_sb[0][32 * q + 4 : 32 * q + 8, :, :].bitcast(I32),
-                )
 
         def word_transposes(src):
             bk = bank("tr")
@@ -115,18 +109,26 @@ def tile_floraperexampleranktworelumlp_x2_kernel(
             A.copy(out=xT[i][:].bitcast(F32), in_=word_transposes(xs[i]))
 
         def consts():
-            A.copy(out=cst[:].bitcast(F32), in_=word_transposes(vecs)[:, :, 0:32, :])
+            src = word_transposes(vecs)
+            for v in range(4):
+                A.copy(out=cst[:, :, 8 * v : 8 * v + 8, :].bitcast(F32), in_=src[:, :, 32 * v : 32 * v + 8, :])
 
         def consts2():
             A.copy(out=cst32[:], in_=cst[:])
-            T.matmul(out=cps[:], lhsT=ident_bf[:], rhs=cst[:].rearrange("p g r t -> p (g r t)"), start=True, stop=True)
+
+        def consts3():
+            A.copy(out=ident_bf[:], in_=ident[:])
+            bk = psum.tile([P, 8, P], BF16, name="bank", tag="bank", bufs=8)
+            for n in range(8):
+                T.transpose(bk[:, n, :], vecs[:, 128 * n : 128 * n + 128], ident_bf[:])
+            A.copy(out=cn32[:], in_=bk[:, :, 96:104])
 
         def xm(i, g):
             h, j = divmod(i, 2)
             V.tensor_tensor(
                 out=mov(0, h, g)[:, 1024 * j : 1024 * j + 1024].rearrange("p (r s t) -> p r s t", r=R, t=4),
                 in0=xT[i][:, g, :, :].unsqueeze(1).to_broadcast([P, R, S, 4]),
-                in1=cpv[:, g, VB1 + 2 * i : VB1 + 2 * i + 2, :].unsqueeze(2).to_broadcast([P, R, S, 4]),
+                in1=cst[:, g, VB1 + 2 * i : VB1 + 2 * i + 2, :].unsqueeze(2).to_broadcast([P, R, S, 4]),
                 op=ALU.mult,
             )
 
@@ -155,8 +157,12 @@ def tile_floraperexampleranktworelumlp_x2_kernel(
                 k = 2 * g + gg
                 T.matmul_mx(
                     out=banks[key][:],
-                    lhsT=w_sb[l][:, k, 256 * t : 256 * t + 256].bitcast(FP4X4),
-                    lhsT_scale=s_sb[l][:, k, 128 * t : 128 * t + 128],
+                    lhsT=(
+                        w_sb[:, k, 256 * t : 256 * t + 256]
+                        if l == 0
+                        else w_raw[1][:, g, 1024 * gg + 256 * t : 1024 * gg + 256 * t + 256]
+                    ).bitcast(FP4X4),
+                    lhsT_scale=s_sb[l][:, 512 * k + 128 * t : 512 * k + 128 * t + 128],
                     rhs=cod(l, h, g)[:].bitcast(FP8X4),
                     rhs_scale=scl(l, h, g)[:],
                     start=(g == 0),
@@ -208,7 +214,7 @@ def tile_floraperexampleranktworelumlp_x2_kernel(
                 out=mv1(h, gg, j, r),
                 in0=res(0, h, gg)[:, j, :, :].rearrange("p t s -> p s t"),
                 scalar=0.0,
-                in1=cpv[:, gg, row : row + 1, :].to_broadcast([P, S, 4]),
+                in1=cst32[:, gg, row : row + 1, :].to_broadcast([P, S, 4]),
                 op0=ALU.max,
                 op1=ALU.mult,
             )
@@ -247,13 +253,86 @@ def tile_floraperexampleranktworelumlp_x2_kernel(
         def ys(h):
             return keep([P, 2, 256], U8, "ys%d" % h)
 
-        def j_(eng, h, gg, j):
-            o = yb(h, gg)[:, 512 * j : 512 * j + 512].rearrange("p (s t) -> p s t", t=4)
-            s = res(1, h, gg)[:, j, :, :].rearrange("p t s -> p s t")
+        def sc_(eng, h, gg, t, r):
+            tm = keep([P, 2, S], F32, "tm%d%d%d%d" % (h, gg, t, r))
+            bk = banks[(1, h, gg, t)]
+            for j in range(2):
+                src = bk[:, 256 * j + 128 * r : 256 * j + 128 * r + 128]
+                c = cn32[:, 4 * gg + t, 2 * (2 * h + j) + r : 2 * (2 * h + j) + r + 1]
+                if eng == "v":
+                    V.tensor_scalar(out=tm[:, j, :], in0=src, scalar1=c, scalar2=None, op0=ALU.mult)
+                else:
+                    A.activation(out=tm[:, j, :], in_=src, func=ACT.Copy, scale=c)
+
+        summed = set()
+
+        def b2_(h, gg, t):
+            summed.add((h, gg, t))
+            src = keep([P, 2, S], F32, "tm%d%d%d0" % (h, gg, t))
+            tm = keep([P, 2, S], F32, "tm%d%d%d1" % (h, gg, t))
+            for j in range(2):
+                V.scalar_tensor_tensor(
+                    out=tm[:, j, :],
+                    in0=banks[(1, h, gg, t)][:, 256 * j + 128 : 256 * j + 256],
+                    scalar=cn32[:, 4 * gg + t, 2 * (2 * h + j) + 1 : 2 * (2 * h + j) + 2],
+                    in1=src[:, j, :],
+                    op0=ALU.mult,
+                    op1=ALU.add,
+                )
+
+        trb = {}
+
+        def rt(h, gg, j):
+            bk = bank("tr")
+            trb[(h, gg, j)] = bk
+            for t in range(4):
+                first = 1 if (h, gg, t) in summed else 0
+                for r in range(first, 2):
+                    tm = keep([P, 2, S], F32, "tm%d%d%d%d" % (h, gg, t, r))
+                    T.matmul(
+                        out=bk[:, 128 * t : 128 * t + 128],
+                        lhsT=tm[:, j, :],
+                        rhs=ident[:],
+                        is_transpose=True,
+                        start=(r == first),
+                        stop=(r == 1),
+                    )
+
+        def os_(h, gg, j):
+            return keep([P, 512], F32, "os%d%d%d" % (h, gg, j))
+
+        def ob_(h, gg, j):
+            return keep([P, 512], BF16, "ob%d%d%d" % (h, gg, j))
+
+        def l_(eng, h, gg, j):
+            if eng == "v":
+                V.tensor_copy(out=os_(h, gg, j)[:], in_=trb[(h, gg, j)][:])
+            else:
+                A.copy(out=os_(h, gg, j)[:], in_=trb[(h, gg, j)][:])
+            nc.sync.dma_start(out=out_0[2 * h + j, :, 512 * gg : 512 * gg + 512], in_=os_(h, gg, j)[:])
+
+        def k_(eng, h, gg, j):
+            if eng == "v":
+                V.tensor_copy(out=ob_(h, gg, j)[:], in_=os_(h, gg, j)[:])
+            elif eng == "g":
+                G_.tensor_copy(out=ob_(h, gg, j)[:], in_=os_(h, gg, j)[:])
+            else:
+                A.copy(out=ob_(h, gg, j)[:], in_=os_(h, gg, j)[:])
+
+        wtb = {}
+
+        def wt(h, gg, j):
+            bk = bank("tr")
+            wtb[(h, gg, j)] = bk
+            w = ob_(h, gg, j)[:].bitcast(F32)
+            for u in range(2):
+                T.transpose(bk[:, 128 * u : 128 * u + 128], w[:, u : 256 : 2], ident[:])
+
+        def y_(eng, h, gg, j):
+            o = yb(h, gg)[:, 512 * j : 512 * j + 512].bitcast(F32).rearrange("p (s u) -> p s u", u=2)
+            s = wtb[(h, gg, j)][:, 0:256].rearrange("p (u s) -> p s u", u=2)
             if eng == "v":
                 V.tensor_copy(out=o, in_=s)
-            elif eng == "g":
-                G_.tensor_scalar(out=o, in0=s, scalar1=1.0, scalar2=1.0, op0=ALU.mult, op1=ALU.mult)
             else:
                 A.copy(out=o, in_=s)
 
@@ -272,245 +351,239 @@ def tile_floraperexampleranktworelumlp_x2_kernel(
                     in_=ys(h)[32 * q : 32 * q + 4, :, :].bitcast(I32),
                 )
 
-        trb = {}
-
-        def rt(h, gg, j, kind="tr"):
-            bk = bank(kind)
-            trb[(h, gg, j)] = bk
-            for t in range(4):
-                T.transpose(bk[:, 128 * t : 128 * t + 128], res(1, h, gg)[:, j, t, :], ident[:])
-
-        def l_(eng, h, gg, j):
-            ot = keep([P, 512], F32, "os%d%d%d" % (h, gg, j))
-            s = trb[(h, gg, j)][:].rearrange("s (t p) -> s p t", t=4)
-            o = ot[:].rearrange("s (p t) -> s p t", t=4)
-            if eng == "v":
-                V.tensor_copy(out=o, in_=s)
-            else:
-                A.copy(out=o, in_=s)
-            nc.sync.dma_start(out=out_0[2 * h + j, :, 512 * gg : 512 * gg + 512], in_=ot[:])
-
         with tc.manual_schedule():
-            G_.memset(vecs[32:64, :].bitcast(U32), 0)
-            G_.memset(vecs[64:128, :].bitcast(U32), 0)
+            G_.memset(vecs[:].bitcast(U32), 0)
             V.memset(s_raw[:].bitcast(I32), 0)
             make_identity(nc, ident[:])
             G_.memset(s_sb[1][:].bitcast(I32), 0)
             w_load(nc.scalar, 0, 0)
-            A.copy(out=ident_bf[:], in_=ident[:])
             nc.sync.dma_start(out=xs[0][:], in_=x[0])
             for k, v in enumerate((b1, a1, b2, a2)):
-                nc.sync.dma_start(out=vecs[8 * k : 8 * k + 8, :], in_=v.rearrange("i r d -> (i r) d"))
+                nc.sync.dma_start(out=vecs[32 * k : 32 * k + 8, :], in_=v.rearrange("i r d -> (i r) d"))
             w_load(nc.sync, 0, 1)
             nc.sync.dma_start(out=xs[1][:], in_=x[1])
-            load_scales(nc.sync, 0)
-            load_scales(nc.sync, 1)
+            load_scales(nc.sync, 0, s_raw)
             nc.sync.dma_start(out=xs[2][:], in_=x[2])
             nc.sync.dma_start(out=xs[3][:], in_=x[3])
+            load_scales(nc.sync, 1, s_sb[1])
             w_load(nc.sync, 1, 0)
             w_load(nc.sync, 1, 1)
+
+            w_perm('v',0,0,0)
             xT_load(0)
             w_perm('v',0,1,0)
             consts()
             xT_load(1)
-            consts2()
-            w_perm('v',0,0,0)
-            xm(0,1)
-            xm(1,1)
-            s_perm()
-            xm(1,0)
+            consts3()
             xT_load(2)
+            w_perm('v',0,0,1)
+            w_perm('v',0,1,1)
             xm(0,0)
-            xm(2,1)
+            consts2()
             xT_load(3)
-            w_perm('g',0,1,1)
-            w_perm('g',0,0,1)
-            xm(3,1)
+            xm(0,1)
+            xm(1,0)
+            xm(1,1)
             quant(0,0,0)
-            xm(2,0)
-            mm(0,0,1,0,(0,))
+            s_perm()
             mm(0,0,1,2,(0,))
+            mm(0,0,0,0,(0,))
             mm(0,0,1,1,(0,))
             quant(0,0,1)
-            w_perm('g',1,0,0)
-            mm(0,0,1,0,(1,))
-            mm(0,0,1,2,(1,))
+            mm(0,0,1,1,(1,))
+            xm(2,0)
+            xm(2,1)
+            xm(3,1)
+            mm(0,0,0,2,(0,))
+            mm(0,0,0,3,(0,))
             xm(3,0)
-            a_(0,0,1,2)
-            mm(0,0,1,3,(0,))
-            mm(0,0,0,1,(0,))
-            mm(0,0,1,3,(1,))
+            a_(0,0,1,1)
+            mm(0,0,0,0,(1,))
             quant(0,1,1)
             quant(0,1,0)
-            mm(0,0,0,0,(0,))
-            mm(0,0,1,1,(1,))
-            mm(0,1,0,0,(0,))
-            a_(0,0,1,0)
-            mm(0,1,0,0,(1,))
-            mm(0,0,0,1,(1,))
-            a_(0,0,1,3)
-            a_(0,0,1,1)
-            b_(0,0,1,0)
-            w_perm('v',1,1,1)
-            b_(0,0,1,2)
-            mm(0,0,0,0,(1,))
-            a_(0,0,0,1)
-            mm(0,1,1,2,(0,))
-            b_(0,0,1,3)
-            mm(0,1,0,1,(0,))
-            a_(0,1,0,0)
-            b_(0,0,1,1)
-            mm(0,1,0,3,(0,))
-            cr(0,1,0,0)
-            mm(0,0,0,3,(0,))
-            mm(0,0,0,3,(1,))
-            mm(0,0,0,2,(0,))
             a_(0,0,0,0)
-            b_(0,0,0,1)
-            mm(0,1,0,1,(1,))
-            w_perm('v',1,1,0)
-            mm(0,0,0,2,(1,))
-            cg1(0,1,0,1)
-            mm(0,1,0,2,(0,))
+            mm(0,0,0,1,(0,))
+            mm(0,0,0,3,(1,))
             a_(0,0,0,3)
-            b_(0,1,0,0)
-            a_(0,0,0,2)
-            b_(0,0,0,3)
+            mm(0,0,1,2,(1,))
+            mm(0,0,0,2,(1,))
+            mm(0,0,1,0,(0,))
+            b_(0,0,1,1)
+            mm(0,0,1,3,(0,))
             b_(0,0,0,0)
+            mm(0,0,0,1,(1,))
+            a_(0,0,0,2)
+            a_(0,0,0,1)
+            mm(0,0,1,0,(1,))
+            mm(0,1,0,0,(0,))
+            mm(0,0,1,3,(1,))
             mm(0,1,1,1,(0,))
+            a_(0,0,1,2)
+            b_(0,0,0,3)
+            a_(0,0,1,0)
             b_(0,0,0,2)
-            cg1(0,1,1,0)
+            b_(0,0,0,1)
+            b_(0,0,1,2)
+            mm(0,1,0,2,(0,))
+            mm(0,1,1,2,(0,))
+            mm(0,1,0,3,(0,))
+            a_(0,0,1,3)
+            cx(0,0,0,0)
             mm(0,1,0,2,(1,))
-            cx(0,1,1,1)
-            mm(0,1,1,0,(0,))
-            mm(0,1,1,1,(1,))
-            mm(0,1,1,3,(0,))
-            mm(0,1,1,0,(1,))
-            cr(0,0,0,0)
-            mm(0,1,0,3,(1,))
-            cr(0,0,1,1)
+            mm(0,1,0,1,(0,))
             a_(0,1,0,2)
-            cr(0,0,1,0)
-            a_(0,1,0,3)
-            b_(0,1,0,3)
-            mm(0,1,1,3,(1,))
-            b_(0,1,0,2)
+            mm(0,1,1,3,(0,))
             mm(0,1,1,2,(1,))
-            cr(0,0,0,1)
-            a_(0,1,0,1)
-            b_(0,1,0,1)
-            w_perm('g',1,0,1)
-            a_(0,1,1,3)
-            quant(1,0,0)
-            quant(1,0,1)
-            a_(0,1,1,1)
+            cx(0,0,0,1)
             a_(0,1,1,2)
-            mm(1,0,1,0,(0,))
-            mm(1,0,0,0,(0,))
+            mm(0,1,1,0,(0,))
+            mm(0,1,0,3,(1,))
+            a_(0,1,0,3)
+            mm(0,1,0,0,(1,))
+            a_(0,1,0,0)
+            mm(0,1,0,1,(1,))
+            b_(0,0,1,0)
+            a_(0,1,0,1)
+            b_(0,0,1,3)
+            cx(0,1,1,0)
+            cr(0,0,1,1)
+            mm(0,1,1,0,(1,))
+            cx(0,0,1,0)
+            mm(0,1,1,3,(1,))
+            cx(0,1,0,1)
+            b_(0,1,0,2)
+            b_(0,1,0,3)
+            cx(0,1,0,0)
+            cx(0,1,1,1)
+            b_(0,1,0,0)
             a_(0,1,1,0)
-            mm(1,0,0,0,(1,))
-            cg1(1,0,0,1)
+            b_(0,1,1,2)
+            quant(1,0,0)
+            a_(0,1,1,3)
+            mm(1,0,1,3,(0,))
+            mm(1,0,0,2,(0,))
+            mm(0,1,1,1,(1,))
+            b_(0,1,0,1)
+            cx(1,0,0,0)
+            quant(1,0,1)
+            mm(1,0,1,1,(0,))
             mm(1,0,0,1,(0,))
+            cr(1,0,1,1)
             mm(1,0,0,1,(1,))
+            sc_('a',0,0,1,1)
+            mm(1,0,1,1,(1,))
+            mm(1,0,1,3,(1,))
+            mm(1,0,0,0,(0,))
+            mm(1,0,0,0,(1,))
+            cr(1,0,0,1)
+            mm(1,0,0,2,(1,))
+            mm(1,0,0,3,(0,))
+            cr(1,0,1,0)
+            b_(0,1,1,0)
+            a_(0,1,1,1)
+            sc_('a',0,0,1,0)
+            mm(1,0,0,3,(1,))
+            mm(1,0,1,0,(0,))
+            quant(1,1,0)
+            sc_('a',0,1,3,0)
+            mm(1,0,1,0,(1,))
             b_(0,1,1,1)
             b_(0,1,1,3)
-            mm(1,0,0,2,(0,))
-            cr(1,0,1,1)
-            a_(1,0,0,0)
-            mm(1,0,1,2,(0,))
-            bg_(1,0,0,0)
-            cr(1,0,1,0)
-            mm(1,0,0,2,(1,))
-            mm(1,0,1,1,(0,))
-            mm(1,0,1,1,(1,))
-            mm(1,0,0,3,(0,))
-            a_(1,0,0,1)
-            cr(1,0,0,0)
-            a_(1,0,0,2)
-            bg_(1,0,0,1)
-            mm(1,0,1,0,(1,))
-            b_(0,1,1,2)
-            quant(1,1,0)
-            a_(1,0,1,1)
-            a_(1,0,1,0)
-            mm(1,0,0,3,(1,))
-            bg_(1,0,0,2)
-            mm(1,0,1,2,(1,))
-            mm(1,0,1,3,(0,))
-            a_(1,0,0,3)
-            mm(1,1,0,0,(0,))
-            mm(1,1,0,3,(0,))
-            mm(1,0,1,3,(1,))
-            bg_(1,0,0,3)
-            rt(0,0,0)
-            rt(0,0,1)
-            bg_(1,0,1,1)
-            mm(1,1,1,0,(0,))
-            a_(1,0,1,2)
-            a_(1,0,1,3)
-            mm(1,1,0,2,(0,))
-            b_(0,1,1,0)
-            cr(1,1,0,0)
-            bg_(1,0,1,2)
-            cr(1,1,1,1)
-            bg_(1,0,1,0)
-            bg_(1,0,1,3)
-            cr(1,1,1,0)
-            cr(1,1,0,1)
-            quant(1,1,1)
-            l_('v',0,0,0)
+            sc_('a',0,0,0,0)
             mm(1,1,1,1,(0,))
-            mm(1,1,1,0,(1,))
-            mm(1,1,0,0,(1,))
-            j_('g',0,1,0)
-            mm(1,1,0,2,(1,))
-            mm(1,1,0,1,(0,))
-            l_('a',0,0,1)
-            j_('a',0,0,1)
-            a_(1,1,1,0)
-            mm(1,1,0,3,(1,))
-            a_(1,1,0,2)
-            j_('a',0,0,0)
-            b_(1,1,0,2)
-            a_(1,1,0,0)
+            sc_('a',0,1,3,1)
+            sc_('a',0,0,0,1)
+            sc_('a',0,1,1,0)
+            mm(1,1,0,3,(0,))
+            b2_(0,1,1)
+            mm(1,1,0,0,(0,))
+            sc_('a',0,0,3,0)
+            b2_(0,0,3)
+            cr(1,1,1,0)
+            mm(1,0,1,2,(0,))
+            sc_('a',0,1,0,1)
+            mm(1,1,0,2,(0,))
+            sc_('a',0,0,2,1)
+            sc_('a',0,0,2,0)
+            cr(1,1,1,1)
+            sc_('a',0,1,0,0)
+            mm(1,0,1,2,(1,))
+            sc_('a',0,1,2,0)
+            sc_('a',0,1,2,1)
+            rt(0,0,1)
+            cr(1,1,0,1)
+            cr(1,1,0,0)
+            rt(0,0,0)
             rt(0,1,0)
-            mm(1,1,0,1,(1,))
-            j_('g',0,1,1)
-            mm(1,1,1,2,(0,))
-            a_(1,1,0,3)
-            l_('v',0,1,0)
-            b_(1,1,0,0)
-            mm(1,1,1,1,(1,))
-            mm(1,1,1,2,(1,))
-            q3(0,0)
-            b_(1,1,0,3)
-            a_(1,1,0,1)
-            a_(1,1,1,1)
-            b_(1,1,0,1)
-            mm(1,1,1,3,(0,))
-            j_('g',1,0,1)
-            a_(1,1,1,2)
-            mm(1,1,1,3,(1,))
             rt(0,1,1)
-            q3(0,1)
-            b_(1,1,1,2)
-            rt(1,0,1,'mm')
-            rt(1,0,0,'mm')
-            a_(1,1,1,3)
+            l_('a',0,0,0)
+            mm(1,1,1,3,(0,))
+            mm(1,1,0,1,(0,))
+            l_('a',0,1,0)
+            quant(1,1,1)
+            mm(1,1,0,2,(1,))
+            k_('v',0,0,0)
             l_('a',0,1,1)
-            l_('a',1,0,1)
-            store_scales(0)
-            l_('a',1,0,0)
-            b_(1,1,1,1)
-            b_(1,1,1,3)
-            b_(1,1,1,0)
-            j_('g',1,1,1)
+            mm(1,1,0,1,(1,))
+            mm(1,1,0,3,(1,))
+            sc_('a',1,0,2,0)
+            l_('a',0,0,1)
+            mm(1,1,1,1,(1,))
+            sc_('a',1,0,1,0)
+            mm(1,1,0,0,(1,))
+            k_('v',0,1,1)
+            b2_(1,0,2)
+            mm(1,1,1,2,(0,))
+            sc_('a',1,0,1,1)
+            sc_('v',1,0,3,0)
+            mm(1,1,1,0,(0,))
+            mm(1,1,1,0,(1,))
+            sc_('a',1,0,0,0)
+            k_('v',0,0,1)
+            mm(1,1,1,3,(1,))
+            mm(1,1,1,2,(1,))
+            b2_(1,0,3)
+            sc_('a',1,1,1,1)
+            sc_('a',1,1,0,0)
+            k_('v',0,1,0)
+            wt(0,0,1)
+            sc_('a',1,1,3,0)
+            b2_(1,0,0)
+            sc_('a',1,1,1,0)
+            wt(0,1,0)
+            sc_('a',1,1,2,1)
+            wt(0,0,0)
+            wt(0,1,1)
+            sc_('a',1,1,2,0)
+            y_('a',0,1,0)
+            y_('a',0,1,1)
+            b2_(1,1,0)
+            b2_(1,1,3)
+            y_('v',0,0,1)
+            y_('v',0,0,0)
+            q3(0,0)
+            rt(1,0,1)
+            q3(0,1)
+            rt(1,0,0)
             rt(1,1,0)
-            j_('g',1,1,0)
-            j_('a',1,0,0)
+            store_scales(0)
+            l_('a',1,0,1)
             l_('v',1,1,0)
+            l_('a',1,0,0)
+            k_('v',1,0,0)
+            k_('a',1,0,1)
             rt(1,1,1)
+            wt(1,0,0)
+            wt(1,0,1)
+            k_('a',1,1,0)
             l_('v',1,1,1)
+            k_('v',1,1,1)
+            y_('v',1,0,0)
+            wt(1,1,0)
+            y_('a',1,0,1)
             q3(1,0)
+            y_('a',1,1,0)
+            wt(1,1,1)
+            y_('a',1,1,1)
             q3(1,1)
             store_scales(1)

from contextlib import ExitStack

import concourse.mybir as mybir
from concourse.masks import make_identity

F32 = mybir.dt.float32
BF16 = mybir.dt.bfloat16
I32 = mybir.dt.int32
U32 = mybir.dt.uint32
U8 = mybir.dt.uint8
FP8X4 = mybir.dt.float8_e4m3fn_x4
FP4X4 = mybir.dt.float4_e2m1fn_x4
ALU = mybir.AluOpType
ACT = mybir.ActivationFunctionType

B, S, R, D, F, E = 4, 128, 2, 1024, 1024, 1024
P = 128
FLOPS = 2 * 2 * B * R * S * D * F
VB1, VA1, VB2, VA2 = 0, 8, 16, 24


def tile_floraperexampleranktworelumlp_x2_kernel(
    tc, x, b1, w1_words, w1_scales, a1, b2, w2_words, w2_scales, a2, out_0, out_1, out_2
):
    nc = tc.nc
    V, A, T, G_ = nc.vector, nc.scalar, nc.tensor, nc.gpsimd
    with ExitStack() as ctx:
        sb = ctx.enter_context(tc.tile_pool(name="sb", bufs=1))
        psum = ctx.enter_context(tc.psum_pool(name="psum", bufs=1))
        made = {}

        def keep(shape, dtype, name):
            if name not in made:
                made[name] = sb.tile(shape, dtype, name=name, tag=name, align_bytes=64)
            return made[name]

        def ring(shape, dtype, tag, bufs):
            return sb.tile(shape, dtype, name=tag, tag=tag, bufs=bufs, align_bytes=64)

        def bank(kind):
            return psum.tile([P, 512], F32, name="bank", tag="bank", bufs=8)

        ident = keep([P, P], F32, "ident")
        ident_bf = keep([P, P], BF16, "identbf")
        cn32 = keep([P, 8, 8], F32, "cn32")
        vecs = keep([P, 1024], BF16, "vecs")
        cst = keep([P, 2, 32, 4], BF16, "cst")
        cst32 = keep([P, 2, 32, 4], F32, "cst32")
        xs = [keep([P, 1024], BF16, "x%d" % i) for i in range(B)]
        xT = [keep([P, 2, S, 4], BF16, "xT%d" % i) for i in range(B)]
        w_raw = [keep([P, 2, 2048], U8, "wraw%d" % l) for l in range(2)]
        s_raw = keep([P, 2048], U8, "sraw")
        w_sb = keep([P, 4, 1024], U8, "w1p")
        s_sb = [keep([P, 2048], U8, "s%d" % l) for l in range(2)]
        words = [w1_words, w2_words]
        scales = [w1_scales, w2_scales]

        def mov(l, h, g):
            return keep([P, 2048], BF16, "mv%d%d%d" % (l, h, g))

        def cod(l, h, g):
            return keep([P, 512], U32, "cd%d%d%d" % (l, h, g))

        def scl(l, h, g):
            return keep([P, 512], U8, "sc%d%d%d" % (l, h, g))

        def res(l, h, g):
            return keep([P, 2, 4, S], F32, "rs%d%d%d" % (l, h, g))

        def load_scales(eng, l, dst):
            for q in range(4):
                eng.dma_start(
                    out=dst[32 * q : 32 * q + 4, :].bitcast(I32).rearrange("p (g n) -> p g n", g=2),
                    in_=scales[l][:, 4 * q : 4 * q + 4, :].rearrange("g r n -> r g n").bitcast(I32),
                )

        def w_load(eng, l, gg):
            eng.dma_start(
                out=w_raw[l][:, :, 1024 * gg : 1024 * gg + 1024].bitcast(I32),
                in_=words[l][:, :, 1024 * gg : 1024 * gg + 1024].rearrange("g p n -> p g n").bitcast(I32),
            )

        def w_perm(eng, l, g, gg):
            o = w_sb[:, 2 * g + gg, :].rearrange("p (t m b) -> p t m b", t=4, b=2)
            s = w_raw[l][:, g, 1024 * gg : 1024 * gg + 1024].rearrange("p (m t b) -> p t m b", t=4, b=2)
            if eng == "v":
                V.tensor_copy(out=o, in_=s)
            else:
                for z in range(2):
                    G_.tensor_copy(out=o[:, 2 * z : 2 * z + 2], in_=s[:, 2 * z : 2 * z + 2])

        def s_perm():
            V.tensor_copy(
                out=s_sb[0][:].rearrange("p (q t m) -> p q t m", q=4, t=4),
                in_=s_raw[:].rearrange("p (q m t) -> p q t m", q=4, t=4),
            )

        def word_transposes(src):
            bk = bank("tr")
            w = src[:].bitcast(F32)
            for g in range(2):
                for u in range(2):
                    T.transpose(
                        bk[:, 128 * (2 * g + u) : 128 * (2 * g + u) + 128], w[:, 256 * g + u : 256 * g + 256 : 2], ident[:]
                    )
            return bk[:].rearrange("p (g u s) -> p g s u", g=2, u=2)

        def xT_load(i):
            A.copy(out=xT[i][:].bitcast(F32), in_=word_transposes(xs[i]))

        def consts():
            src = word_transposes(vecs)
            for v in range(4):
                A.copy(out=cst[:, :, 8 * v : 8 * v + 8, :].bitcast(F32), in_=src[:, :, 32 * v : 32 * v + 8, :])

        def consts2():
            A.copy(out=cst32[:], in_=cst[:])

        def consts3():
            A.copy(out=ident_bf[:], in_=ident[:])
            bk = psum.tile([P, 8, P], BF16, name="bank", tag="bank", bufs=8)
            for n in range(8):
                T.transpose(bk[:, n, :], vecs[:, 128 * n : 128 * n + 128], ident_bf[:])
            A.copy(out=cn32[:], in_=bk[:, :, 96:104])

        def xm(i, g):
            h, j = divmod(i, 2)
            V.tensor_tensor(
                out=mov(0, h, g)[:, 1024 * j : 1024 * j + 1024].rearrange("p (r s t) -> p r s t", r=R, t=4),
                in0=xT[i][:, g, :, :].unsqueeze(1).to_broadcast([P, R, S, 4]),
                in1=cst[:, g, VB1 + 2 * i : VB1 + 2 * i + 2, :].unsqueeze(2).to_broadcast([P, R, S, 4]),
                op=ALU.mult,
            )

        def xg(i, g):
            h, j = divmod(i, 2)
            for r in range(2):
                for z in range(2):
                    o = 1024 * j + 512 * r + 256 * z
                    G_.tensor_tensor(
                        out=mov(0, h, g)[:, o : o + 256].rearrange("p (s t) -> p s t", t=4),
                        in0=xT[i][:, g, 64 * z : 64 * z + 64, :],
                        in1=cst[:, g, VB1 + 2 * i + r : VB1 + 2 * i + r + 1, :].to_broadcast([P, 64, 4]),
                        op=ALU.mult,
                    )

        def quant(l, h, g):
            V.quantize_mx(out=cod(l, h, g)[:].bitcast(FP8X4), scales=scl(l, h, g)[:], in_=mov(l, h, g)[:])

        banks = {}

        def mm(l, h, gg, t, gs):
            key = (l, h, gg, t)
            if gs[0] == 0:
                banks[key] = bank("mm")
            for g in gs:
                k = 2 * g + gg
                T.matmul_mx(
                    out=banks[key][:],
                    lhsT=(
                        w_sb[:, k, 256 * t : 256 * t + 256]
                        if l == 0
                        else w_raw[1][:, g, 1024 * gg + 256 * t : 1024 * gg + 256 * t + 256]
                    ).bitcast(FP4X4),
                    lhsT_scale=s_sb[l][:, 512 * k + 128 * t : 512 * k + 128 * t + 128],
                    rhs=cod(l, h, g)[:].bitcast(FP8X4),
                    rhs_scale=scl(l, h, g)[:],
                    start=(g == 0),
                    stop=(g == 1),
                )

        tmps = {}

        def col(vec, i, r, gg, t):
            return cst32[:, gg, vec + 2 * i + r, t : t + 1]

        def scaled(l, h, gg, t, r, tag, bufs):
            tmp = ring([P, 2, S], F32, tag, bufs)
            bk = banks[(l, h, gg, t)]
            for j in range(2):
                A.activation(
                    out=tmp[:, j, :],
                    in_=bk[:, 256 * j + 128 * r : 256 * j + 128 * r + 128],
                    func=ACT.Copy,
                    scale=col(VA1 if l == 0 else VA2, 2 * h + j, r, gg, t),
                )
            return tmp

        def a_(l, h, gg, t):
            tmps[(l, h, gg, t)] = scaled(l, h, gg, t, 0, "tmp", 16)

        def b_(l, h, gg, t):
            for j in range(2):
                V.scalar_tensor_tensor(
                    out=res(l, h, gg)[:, j, t, :],
                    in0=banks[(l, h, gg, t)][:, 256 * j + 128 : 256 * j + 256],
                    scalar=col(VA1 if l == 0 else VA2, 2 * h + j, 1, gg, t),
                    in1=tmps[(l, h, gg, t)][:, j, :],
                    op0=ALU.mult,
                    op1=ALU.add,
                )

        def bg_(l, h, gg, t):
            tm1 = scaled(l, h, gg, t, 1, "tm1", 8)
            G_.tensor_tensor(out=res(l, h, gg)[:, :, t, :], in0=tmps[(l, h, gg, t)][:], in1=tm1[:], op=ALU.add)

        def mv1(h, gg, j, r):
            o = 1024 * j + 512 * r
            return mov(1, h, gg)[:, o : o + 512].rearrange("p (s t) -> p s t", t=4)

        def cr(h, gg, j, r):
            row = VB2 + 2 * (2 * h + j) + r
            V.scalar_tensor_tensor(
                out=mv1(h, gg, j, r),
                in0=res(0, h, gg)[:, j, :, :].rearrange("p t s -> p s t"),
                scalar=0.0,
                in1=cst32[:, gg, row : row + 1, :].to_broadcast([P, S, 4]),
                op0=ALU.max,
                op1=ALU.mult,
            )

        def cx(h, gg, j, r):
            pl = keep([P, 4, S], BF16, "pl%d%d%d%d" % (h, gg, j, r))
            for t in range(4):
                V.tensor_scalar(
                    out=pl[:, t, :],
                    in0=res(0, h, gg)[:, j, t, :],
                    scalar1=0.0,
                    scalar2=col(VB2, 2 * h + j, r, gg, t),
                    op0=ALU.max,
                    op1=ALU.mult,
                )
            A.copy(out=mv1(h, gg, j, r), in_=pl[:].rearrange("p t s -> p s t"))

        def cg1(h, gg, j, r):
            name = "hi%d%d%d" % (h, gg, j)
            new = name not in made
            hi = keep([P, S, 4], F32, name)
            if new:
                A.activation(out=hi[:], in_=res(0, h, gg)[:, j, :, :].rearrange("p t s -> p s t"), func=ACT.Relu)
            row = VB2 + 2 * (2 * h + j) + r
            for z in range(2):
                G_.tensor_tensor(
                    out=mv1(h, gg, j, r)[:, 64 * z : 64 * z + 64, :],
                    in0=hi[:, 64 * z : 64 * z + 64, :],
                    in1=cst32[:, gg, row : row + 1, :].to_broadcast([P, 64, 4]),
                    op=ALU.mult,
                )

        def yb(h, gg):
            return keep([P, 1024], BF16, "yb%d%d" % (h, gg))

        def ys(h):
            return keep([P, 2, 256], U8, "ys%d" % h)

        def sc_(eng, h, gg, t, r):
            tm = keep([P, 2, S], F32, "tm%d%d%d%d" % (h, gg, t, r))
            bk = banks[(1, h, gg, t)]
            for j in range(2):
                src = bk[:, 256 * j + 128 * r : 256 * j + 128 * r + 128]
                c = cn32[:, 4 * gg + t, 2 * (2 * h + j) + r : 2 * (2 * h + j) + r + 1]
                if eng == "v":
                    V.tensor_scalar(out=tm[:, j, :], in0=src, scalar1=c, scalar2=None, op0=ALU.mult)
                else:
                    A.activation(out=tm[:, j, :], in_=src, func=ACT.Copy, scale=c)

        summed = set()

        def b2_(h, gg, t):
            summed.add((h, gg, t))
            src = keep([P, 2, S], F32, "tm%d%d%d0" % (h, gg, t))
            tm = keep([P, 2, S], F32, "tm%d%d%d1" % (h, gg, t))
            for j in range(2):
                V.scalar_tensor_tensor(
                    out=tm[:, j, :],
                    in0=banks[(1, h, gg, t)][:, 256 * j + 128 : 256 * j + 256],
                    scalar=cn32[:, 4 * gg + t, 2 * (2 * h + j) + 1 : 2 * (2 * h + j) + 2],
                    in1=src[:, j, :],
                    op0=ALU.mult,
                    op1=ALU.add,
                )

        trb = {}

        def rt(h, gg, j):
            bk = bank("tr")
            trb[(h, gg, j)] = bk
            for t in range(4):
                first = 1 if (h, gg, t) in summed else 0
                for r in range(first, 2):
                    tm = keep([P, 2, S], F32, "tm%d%d%d%d" % (h, gg, t, r))
                    T.matmul(
                        out=bk[:, 128 * t : 128 * t + 128],
                        lhsT=tm[:, j, :],
                        rhs=ident[:],
                        is_transpose=True,
                        start=(r == first),
                        stop=(r == 1),
                    )

        def os_(h, gg, j):
            return keep([P, 512], F32, "os%d%d%d" % (h, gg, j))

        def ob_(h, gg, j):
            return keep([P, 512], BF16, "ob%d%d%d" % (h, gg, j))

        def l_(eng, h, gg, j):
            if eng == "v":
                V.tensor_copy(out=os_(h, gg, j)[:], in_=trb[(h, gg, j)][:])
            else:
                A.copy(out=os_(h, gg, j)[:], in_=trb[(h, gg, j)][:])
            nc.sync.dma_start(out=out_0[2 * h + j, :, 512 * gg : 512 * gg + 512], in_=os_(h, gg, j)[:])

        def k_(eng, h, gg, j):
            if eng == "v":
                V.tensor_copy(out=ob_(h, gg, j)[:], in_=os_(h, gg, j)[:])
            elif eng == "g":
                G_.tensor_copy(out=ob_(h, gg, j)[:], in_=os_(h, gg, j)[:])
            else:
                A.copy(out=ob_(h, gg, j)[:], in_=os_(h, gg, j)[:])

        wtb = {}

        def wt(h, gg, j):
            bk = bank("tr")
            wtb[(h, gg, j)] = bk
            w = ob_(h, gg, j)[:].bitcast(F32)
            for u in range(2):
                T.transpose(bk[:, 128 * u : 128 * u + 128], w[:, u : 256 : 2], ident[:])

        def y_(eng, h, gg, j):
            o = yb(h, gg)[:, 512 * j : 512 * j + 512].bitcast(F32).rearrange("p (s u) -> p s u", u=2)
            s = wtb[(h, gg, j)][:, 0:256].rearrange("p (u s) -> p s u", u=2)
            if eng == "v":
                V.tensor_copy(out=o, in_=s)
            else:
                A.copy(out=o, in_=s)

        def q3(h, gg):
            yc = keep([P, 256], U32, "yc%d%d" % (h, gg))
            V.quantize_mx(out=yc[:].bitcast(FP8X4), scales=ys(h)[:, gg, :], in_=yb(h, gg)[:])
            nc.sync.dma_start(
                out=out_1[gg, :, 256 * h : 256 * h + 256, :].rearrange("p m b -> p (m b)").bitcast(I32),
                in_=yc[:].bitcast(I32),
            )

        def store_scales(h):
            for q in range(4):
                nc.sync.dma_start(
                    out=out_2[:, 4 * q : 4 * q + 4, 256 * h : 256 * h + 256].rearrange("g q m -> q g m").bitcast(I32),
                    in_=ys(h)[32 * q : 32 * q + 4, :, :].bitcast(I32),
                )

        with tc.manual_schedule():
            G_.memset(vecs[:].bitcast(U32), 0)
            V.memset(s_raw[:].bitcast(I32), 0)
            make_identity(nc, ident[:])
            G_.memset(s_sb[1][:].bitcast(I32), 0)
            w_load(nc.scalar, 0, 0)
            nc.sync.dma_start(out=xs[0][:], in_=x[0])
            for k, v in enumerate((b1, a1, b2, a2)):
                nc.sync.dma_start(out=vecs[32 * k : 32 * k + 8, :], in_=v.rearrange("i r d -> (i r) d"))
            w_load(nc.sync, 0, 1)
            nc.sync.dma_start(out=xs[1][:], in_=x[1])
            load_scales(nc.sync, 0, s_raw)
            nc.sync.dma_start(out=xs[2][:], in_=x[2])
            nc.sync.dma_start(out=xs[3][:], in_=x[3])
            load_scales(nc.sync, 1, s_sb[1])
            w_load(nc.sync, 1, 0)
            w_load(nc.sync, 1, 1)

            w_perm('v',0,0,0)
            xT_load(0)
            w_perm('v',0,1,0)
            consts()
            xT_load(1)
            consts3()
            xT_load(2)
            w_perm('v',0,0,1)
            w_perm('v',0,1,1)
            xm(0,0)
            consts2()
            xT_load(3)
            xm(0,1)
            xm(1,0)
            xm(1,1)
            quant(0,0,0)
            s_perm()
            mm(0,0,1,2,(0,))
            mm(0,0,0,0,(0,))
            mm(0,0,1,1,(0,))
            quant(0,0,1)
            mm(0,0,1,1,(1,))
            xm(2,0)
            xm(2,1)
            xm(3,1)
            mm(0,0,0,2,(0,))
            mm(0,0,0,3,(0,))
            xm(3,0)
            a_(0,0,1,1)
            mm(0,0,0,0,(1,))
            quant(0,1,1)
            quant(0,1,0)
            a_(0,0,0,0)
            mm(0,0,0,1,(0,))
            mm(0,0,0,3,(1,))
            a_(0,0,0,3)
            mm(0,0,1,2,(1,))
            mm(0,0,0,2,(1,))
            mm(0,0,1,0,(0,))
            b_(0,0,1,1)
            mm(0,0,1,3,(0,))
            b_(0,0,0,0)
            mm(0,0,0,1,(1,))
            a_(0,0,0,2)
            a_(0,0,0,1)
            mm(0,0,1,0,(1,))
            mm(0,1,0,0,(0,))
            mm(0,0,1,3,(1,))
            mm(0,1,1,1,(0,))
            a_(0,0,1,2)
            b_(0,0,0,3)
            a_(0,0,1,0)
            b_(0,0,0,2)
            b_(0,0,0,1)
            b_(0,0,1,2)
            mm(0,1,0,2,(0,))
            mm(0,1,1,2,(0,))
            mm(0,1,0,3,(0,))
            a_(0,0,1,3)
            cx(0,0,0,0)
            mm(0,1,0,2,(1,))
            mm(0,1,0,1,(0,))
            a_(0,1,0,2)
            mm(0,1,1,3,(0,))
            mm(0,1,1,2,(1,))
            cx(0,0,0,1)
            a_(0,1,1,2)
            mm(0,1,1,0,(0,))
            mm(0,1,0,3,(1,))
            a_(0,1,0,3)
            mm(0,1,0,0,(1,))
            a_(0,1,0,0)
            mm(0,1,0,1,(1,))
            b_(0,0,1,0)
            a_(0,1,0,1)
            b_(0,0,1,3)
            cx(0,1,1,0)
            cr(0,0,1,1)
            mm(0,1,1,0,(1,))
            cx(0,0,1,0)
            mm(0,1,1,3,(1,))
            cx(0,1,0,1)
            b_(0,1,0,2)
            b_(0,1,0,3)
            cx(0,1,0,0)
            cx(0,1,1,1)
            b_(0,1,0,0)
            a_(0,1,1,0)
            b_(0,1,1,2)
            quant(1,0,0)
            a_(0,1,1,3)
            mm(1,0,1,3,(0,))
            mm(1,0,0,2,(0,))
            mm(0,1,1,1,(1,))
            b_(0,1,0,1)
            cx(1,0,0,0)
            quant(1,0,1)
            mm(1,0,1,1,(0,))
            mm(1,0,0,1,(0,))
            cr(1,0,1,1)
            mm(1,0,0,1,(1,))
            sc_('a',0,0,1,1)
            mm(1,0,1,1,(1,))
            mm(1,0,1,3,(1,))
            mm(1,0,0,0,(0,))
            mm(1,0,0,0,(1,))
            cr(1,0,0,1)
            mm(1,0,0,2,(1,))
            mm(1,0,0,3,(0,))
            cr(1,0,1,0)
            b_(0,1,1,0)
            a_(0,1,1,1)
            sc_('a',0,0,1,0)
            mm(1,0,0,3,(1,))
            mm(1,0,1,0,(0,))
            quant(1,1,0)
            sc_('a',0,1,3,0)
            mm(1,0,1,0,(1,))
            b_(0,1,1,1)
            b_(0,1,1,3)
            sc_('a',0,0,0,0)
            mm(1,1,1,1,(0,))
            sc_('a',0,1,3,1)
            sc_('a',0,0,0,1)
            sc_('a',0,1,1,0)
            mm(1,1,0,3,(0,))
            b2_(0,1,1)
            mm(1,1,0,0,(0,))
            sc_('a',0,0,3,0)
            b2_(0,0,3)
            cr(1,1,1,0)
            mm(1,0,1,2,(0,))
            sc_('a',0,1,0,1)
            mm(1,1,0,2,(0,))
            sc_('a',0,0,2,1)
            sc_('a',0,0,2,0)
            cr(1,1,1,1)
            sc_('a',0,1,0,0)
            mm(1,0,1,2,(1,))
            sc_('a',0,1,2,0)
            sc_('a',0,1,2,1)
            rt(0,0,1)
            cr(1,1,0,1)
            cr(1,1,0,0)
            rt(0,0,0)
            rt(0,1,0)
            rt(0,1,1)
            l_('a',0,0,0)
            mm(1,1,1,3,(0,))
            mm(1,1,0,1,(0,))
            l_('a',0,1,0)
            quant(1,1,1)
            mm(1,1,0,2,(1,))
            k_('v',0,0,0)
            l_('a',0,1,1)
            mm(1,1,0,1,(1,))
            mm(1,1,0,3,(1,))
            sc_('a',1,0,2,0)
            l_('a',0,0,1)
            mm(1,1,1,1,(1,))
            sc_('a',1,0,1,0)
            mm(1,1,0,0,(1,))
            k_('v',0,1,1)
            b2_(1,0,2)
            mm(1,1,1,2,(0,))
            sc_('a',1,0,1,1)
            sc_('v',1,0,3,0)
            mm(1,1,1,0,(0,))
            mm(1,1,1,0,(1,))
            sc_('a',1,0,0,0)
            k_('v',0,0,1)
            mm(1,1,1,3,(1,))
            mm(1,1,1,2,(1,))
            b2_(1,0,3)
            sc_('a',1,1,1,1)
            sc_('a',1,1,0,0)
            k_('v',0,1,0)
            wt(0,0,1)
            sc_('a',1,1,3,0)
            b2_(1,0,0)
            sc_('a',1,1,1,0)
            wt(0,1,0)
            sc_('a',1,1,2,1)
            wt(0,0,0)
            wt(0,1,1)
            sc_('a',1,1,2,0)
            y_('a',0,1,0)
            y_('a',0,1,1)
            b2_(1,1,0)
            b2_(1,1,3)
            y_('v',0,0,1)
            y_('v',0,0,0)
            q3(0,0)
            rt(1,0,1)
            q3(0,1)
            rt(1,0,0)
            rt(1,1,0)
            store_scales(0)
            l_('a',1,0,1)
            l_('v',1,1,0)
            l_('a',1,0,0)
            k_('v',1,0,0)
            k_('a',1,0,1)
            rt(1,1,1)
            wt(1,0,0)
            wt(1,0,1)
            k_('a',1,1,0)
            l_('v',1,1,1)
            k_('v',1,1,1)
            y_('v',1,0,0)
            wt(1,1,0)
            y_('a',1,0,1)
            q3(1,0)
            y_('a',1,1,0)
            wt(1,1,1)
            y_('a',1,1,1)
            q3(1,1)
            store_scales(1)
